import numpy as np
import ml_dtypes


def mxq(x, axis, fmt="e4m3"):
    dtype, down = {"e4m3": (ml_dtypes.float8_e4m3fn, 7), "e5m2": (ml_dtypes.float8_e5m2, 14)}[fmt]
    v = np.moveaxis(np.asarray(x, np.float32).astype(ml_dtypes.bfloat16).astype(np.float64), axis, -1)
    blocks = v.reshape(v.shape[:-1] + (-1, 32))
    amax = np.abs(blocks).max(-1, keepdims=True)
    byte = np.maximum(np.where(amax > 0, np.frexp(amax)[1] - 1 + 127, 0) - down, 1)
    scale = np.exp2(byte - 127.0)
    codes = (blocks / scale).astype(np.float32).astype(dtype).astype(np.float64)
    return np.moveaxis((codes * scale).reshape(v.shape), -1, axis)


WIDE = False


def mx_kscale(k):
    if not WIDE:
        return np.ones(k)
    levels = np.array([10, -10, 5, -5, 0])
    if k % 512:
        return np.exp2(np.random.permutation(np.resize(levels, k // 32))).repeat(32)
    a = np.empty((k // 512, 16))
    for p in range(k // 512):
        a[p, :8] = np.random.permutation(np.resize(levels, 8))
        for g in range(8):
            far = levels[np.abs(levels - a[p, g]) >= 10]
            a[p, g + 8] = far[np.random.randint(len(far))]
    return np.exp2(a.ravel()).repeat(32)


def f64(x):
    return np.asarray(x).astype(np.float64)


def striped(idx):
    return np.tile(idx.reshape(-1, 16).T, (8, 1)).astype(np.uint16)


def unstriped(offs):
    return offs[:16].T.reshape(-1).astype(np.int64)


E2M1 = np.array([0.0, 0.5, 1.0, 1.5, 2.0, 3.0, 4.0, 6.0, -0.0, -0.5, -1.0, -1.5, -2.0, -3.0, -4.0, -6.0])


def pack_fp4(w):
    k, n = w.shape
    w = f64(np.asarray(w, np.float32).astype(ml_dtypes.bfloat16)).reshape(k // 32, 32, n)
    amax = np.abs(w).max(1)
    mant, ex = np.frexp(amax / 6.0)
    byte = np.clip(np.where(amax > 0, np.where(mant > 0.5, ex, ex - 1) + 127, 1), 1, 254)
    scaled = (w * np.exp2(127.0 - byte)[:, None, :]).reshape(k, n).astype(np.float32)
    c = np.ascontiguousarray(scaled.reshape(k // 512, 128, 4, n).transpose(0, 1, 3, 2)).astype(ml_dtypes.float4_e2m1fn).view(np.uint8) & 0xF
    words = (c[..., 0::2] | (c[..., 1::2] << 4)).reshape(k // 512, 128, 2 * n)
    return np.ascontiguousarray(words), np.ascontiguousarray(byte.astype(np.uint8).reshape(k // 512, 16, n))


def unpack_fp4(words, scales):
    g, _, n = scales.shape
    words = np.ascontiguousarray(words).reshape(g, 128, n, 2)
    nib = np.empty((g, 128, n, 4), np.uint8)
    nib[..., 0::2] = words & 0xF
    nib[..., 1::2] = words >> 4
    vals = E2M1[nib] * np.repeat(np.exp2(scales.astype(np.float64) - 127.0), 8, axis=1)[..., None]
    return vals.transpose(0, 1, 3, 2).reshape(g * 512, n)


def relu(v):
    return np.maximum(v, 0.0)


K, T, S, V, H, N = 1024, 2048, 768, 256, 512, 128


def setup_inputs():
    n = np.random.standard_normal
    s = mx_kscale(K)[:, None]
    u = mx_kscale(H)
    packed_w4 = pack_fp4(n((H, N)) / np.sqrt(H) / u[:, None])
    return {
        "xT": (n((K, T)) * s).astype(np.float32),
        "w1": (n((K, H)) / np.sqrt(K) / s * u).astype(np.float32),
        "w2": (n((K, H)) / np.sqrt(K) / s).astype(np.float32),
        "w3": (n((K, H)) / np.sqrt(K) / s).astype(np.float32),
        "w4_words": packed_w4[0],
        "w4_scales": packed_w4[1],
        "offs": striped(np.random.permutation(T)[:S]),
    }


def reference(xT, w1, w2, w3, w4_words, w4_scales, offs):
    xq = mxq(f64(xT)[:, unstriped(offs)], 0, "e4m3")
    z = (((mxq(f64(w1), 0, "e4m3").T @ xq[:, :V])) * ((mxq(f64(w2), 0, "e4m3").T @ xq[:, V:2 * V]))) * ((mxq(f64(w3), 0, "e4m3").T @ xq[:, 2 * V:3 * V]))
    return relu(unpack_fp4(w4_words, w4_scales).T @ mxq(z, 0, "e4m3"))

@@ -1,0 +1,199 @@
+from contextlib import ExitStack
+
+import concourse.mybir as mybir
+
+K, T, V, H, N = 1024, 2048, 256, 512, 128
+PIECES = 3
+FLOPS = 2 * PIECES * K * H * V + 2 * H * N * V
+
+F32 = mybir.dt.float32
+BF16 = mybir.dt.bfloat16
+I32 = mybir.dt.int32
+U32 = mybir.dt.uint32
+U16 = mybir.dt.uint16
+U8 = mybir.dt.uint8
+FP8X4 = mybir.dt.float8_e4m3fn_x4
+FP4X4 = mybir.dt.float4_e2m1fn_x4
+MULT = mybir.AluOpType.mult
+RELU = mybir.ActivationFunctionType.Relu
+
+P = 128
+PACK = 4
+K_PASS = P * PACK
+PASSES = K // K_PASS
+S = PIECES * V
+HALF = V // 2
+LIST_ROWS = 16
+RUN = 4
+
+
+def tile_picked_trilin_relu_e_kernel(tc, xT, w1, w2, w3, w4_words, w4_scales, offs, out):
+    nc = tc.nc
+    weights = (w1, w2, w3)
+
+    with ExitStack() as ctx:
+        keep = ctx.enter_context(tc.tile_pool(name="keep", bufs=1))
+        psum = ctx.enter_context(tc.psum_pool(name="psum", bufs=1))
+
+        def sb(name, shape, dtype):
+            return keep.tile(shape, dtype, name=name, align_bytes=64)
+
+        offsets = keep.tile([P, S // LIST_ROWS], U16, name="offsets")
+        nc.sync.dma_start(offsets[:], offs)
+
+        w4_codes = sb("w4_codes", [P, 2 * N], U8)
+        w4_scale = sb("w4_scale", [P, N], U8)
+        nc.gpsimd.memset(w4_scale[:], 0)
+        nc.gpsimd.dma_start(w4_codes[:].bitcast(I32), w4_words[0].bitcast(I32))
+        for q in range(4):
+            nc.gpsimd.dma_start(w4_scale[32 * q : 32 * q + 4, :].bitcast(I32), w4_scales[0, 4 * q : 4 * q + 4, :].bitcast(I32))
+
+        x_plane = {}
+        for g in range(PASSES):
+            rows = xT[g * K_PASS : (g + 1) * K_PASS, :].rearrange("(p j) c -> p j c", j=PACK)
+            for j in range(PACK):
+                x_plane[g, j] = sb("x_plane%d%d" % (g, j), [P, T], F32)
+                nc.sync.dma_start(x_plane[g, j][:], rows[:, j, :])
+        w_raw = {}
+        for d in range(PIECES):
+            for g in range(PASSES):
+                rows = weights[d][g * K_PASS : (g + 1) * K_PASS, :].rearrange("(p j) c -> p j c", j=PACK)
+                last = d == PIECES - 1 and g == PASSES - 1
+                cuts = [0, 256, H] if last else [0, H]
+                w_raw[d, g] = []
+                for a, b in zip(cuts, cuts[1:]):
+                    raw = sb("w_raw%d%d_%d" % (d, g, a), [P, PACK, b - a], F32)
+                    nc.sync.dma_start(raw[:], rows[:, :, a:b])
+                    w_raw[d, g].append((a, b, raw))
+
+        picked = {g: sb("picked%d" % g, [P, PACK, S], BF16) for g in range(PASSES)}
+        x_woven, x_codes, x_scale = {}, {}, {}
+        w_woven, w_codes, w_scale = {}, {}, {}
+        for d in range(PIECES):
+            for g in range(PASSES):
+                x_woven[d, g] = sb("x_woven%d%d" % (d, g), [P, V, PACK], BF16)
+                x_codes[d, g] = sb("x_codes%d%d" % (d, g), [P, V], U32)
+                x_scale[d, g] = sb("x_scale%d%d" % (d, g), [P, V], U8)
+                w_woven[d, g] = sb("w_woven%d%d" % (d, g), [P, PACK, P, PACK], BF16)
+                w_codes[d, g] = sb("w_codes%d%d" % (d, g), [P, H], U32)
+                w_scale[d, g] = sb("w_scale%d%d" % (d, g), [P, H], U8)
+
+        def gather(g, j, a, b):
+            nc.vector.tensor_copy(picked[g][:, j, a:b], x_plane[g, j][:].indirect(offsets[:, a // LIST_ROWS : b // LIST_ROWS]))
+
+        def weave_x(d, g):
+            nc.scalar.copy(
+                x_woven[d, g][:].rearrange("p (c i) j -> p c j i", i=RUN),
+                picked[g][:, :, d * V : (d + 1) * V].rearrange("p j (c i) -> p c j i", i=RUN),
+            )
+
+        def quantize_x(d, g):
+            nc.vector.quantize_mx(
+                out=x_codes[d, g][:].bitcast(FP8X4),
+                scales=x_scale[d, g][:],
+                in_=x_woven[d, g][:].rearrange("p v j -> p (v j)"),
+            )
+
+        def weave_w(copy, d, g, a, b):
+            for lo, hi, raw in w_raw[d, g]:
+                if lo <= a and b <= hi:
+                    copy(
+                        w_woven[d, g][:, :, a // PACK : b // PACK, :].rearrange("p t m j -> p m j t"),
+                        raw[:, :, a - lo : b - lo].rearrange("p j (m t) -> p m j t", t=PACK),
+                    )
+
+        def quantize_w(d, g, t0, t1):
+            nc.vector.quantize_mx(
+                out=w_codes[d, g][:, t0 * P : t1 * P].bitcast(FP8X4),
+                scales=w_scale[d, g][:, t0 * P : t1 * P],
+                in_=w_woven[d, g][:, t0:t1, :, :].rearrange("p t m j -> p (t m j)"),
+            )
+
+        y = {(d, h): psum.tile([P, PACK, HALF], F32, name="y%d%d" % (d, h)) for d in range(PIECES) for h in range(2)}
+
+        def product(d, h):
+            cols = slice(h * HALF, (h + 1) * HALF)
+            for t in range(PACK):
+                chans = slice(t * P, (t + 1) * P)
+                for g in range(PASSES):
+                    nc.tensor.matmul_mx(
+                        out=y[d, h][:, t, :],
+                        lhsT=w_codes[d, g][:, chans].bitcast(FP8X4),
+                        lhsT_scale=w_scale[d, g][:, chans],
+                        rhs=x_codes[d, g][:, cols].bitcast(FP8X4),
+                        rhs_scale=x_scale[d, g][:, cols],
+                        start=(g == 0),
+                        stop=(g == PASSES - 1),
+                    )
+
+        def by_triple(d, h):
+            return y[d, h][:].rearrange("p t v -> p v t")
+
+        on_vector, on_scalar = nc.vector.tensor_copy, nc.scalar.copy
+        y1 = [sb("y1_%d" % h, [P, HALF, PACK], F32) for h in range(2)]
+        y12 = [sb("y12_%d" % h, [P, HALF, PACK], F32) for h in range(2)]
+        z = [sb("z%d" % h, [P, HALF, PACK], BF16) for h in range(2)]
+        z_codes = [sb("z_codes%d" % h, [P, HALF], U32) for h in range(2)]
+        z_scale = [sb("z_scale%d" % h, [P, HALF], U8) for h in range(2)]
+        res = [sb("res%d" % h, [P, HALF], F32) for h in range(2)]
+        acc = [psum.tile([P, HALF], F32, name="acc%d" % h) for h in range(2)]
+
+        for j in range(PACK):
+            gather(0, j, 0, S)
+        for d in range(PIECES):
+            weave_x(d, 0)
+        for j in range(PACK - 1):
+            gather(1, j, 0, S)
+            quantize_x(j, 0)
+        for d in range(PIECES):
+            gather(1, PACK - 1, d * V, (d + 1) * V)
+            weave_x(d, 1)
+        weave_w(on_vector, 0, 0, 0, H)
+        quantize_x(0, 1)
+        quantize_w(0, 0, 0, PACK)
+        weave_w(on_vector, 0, 1, 0, H)
+        quantize_x(1, 1)
+        quantize_x(2, 1)
+        quantize_w(0, 1, 0, PACK)
+        product(0, 0)
+        product(0, 1)
+        weave_w(on_scalar, 1, 0, 0, 256)
+        weave_w(on_vector, 1, 0, 256, H)
+        quantize_w(1, 0, 0, PACK)
+        for h in range(2):
+            nc.scalar.copy(y1[h][:], by_triple(0, h))
+        weave_w(on_scalar, 1, 1, 0, 128)
+        weave_w(on_vector, 1, 1, 128, H)
+        quantize_w(1, 1, 0, 2)
+        quantize_w(1, 1, 2, 4)
+        product(1, 0)
+        product(1, 1)
+        weave_w(on_scalar, 2, 0, 0, 256)
+        weave_w(on_vector, 2, 0, 256, H)
+        nc.vector.tensor_tensor(y12[0][:], by_triple(1, 0), y1[0][:], MULT)
+        quantize_w(2, 0, 0, PACK)
+        nc.vector.tensor_tensor(y12[1][:], by_triple(1, 1), y1[1][:], MULT)
+        weave_w(on_scalar, 2, 1, 0, 256)
+        weave_w(on_scalar, 2, 1, 256, 320)
+        weave_w(on_vector, 2, 1, 320, H)
+        for t in range(PACK):
+            quantize_w(2, 1, t, t + 1)
+        product(2, 0)
+        product(2, 1)
+        for h in range(2):
+            nc.vector.tensor_tensor(z[h][:], by_triple(2, h), y12[h][:], MULT)
+        for h in range(2):
+            nc.vector.quantize_mx(out=z_codes[h][:].bitcast(FP8X4), scales=z_scale[h][:], in_=z[h][:].rearrange("p v t -> p (v t)"))
+            nc.tensor.matmul_mx(
+                out=acc[h][:],
+                lhsT=w4_codes[:].bitcast(FP4X4),
+                lhsT_scale=w4_scale[:],
+                rhs=z_codes[h][:].bitcast(FP8X4),
+                rhs_scale=z_scale[h][:],
+                start=True,
+                stop=True,
+            )
+        nc.scalar.activation(res[0][:], acc[0][:], RELU)
+        nc.scalar.dma_start(out[:, 0:HALF], res[0][:])
+        nc.vector.tensor_scalar_max(res[1][:], acc[1][:], 0.0)
+        nc.sync.dma_start(out[:, HALF:V], res[1][:])

@@ -35,18 +35,17 @@ def tile_picked_trilin_relu_e_kernel(tc, xT, w1, w2, w3, w4_words, w4_scales, of
         keep = ctx.enter_context(tc.tile_pool(name="keep", bufs=1))
         psum = ctx.enter_context(tc.psum_pool(name="psum", bufs=1))
 
-        def sb(name, shape, dtype):
-            return keep.tile(shape, dtype, name=name, align_bytes=64)
+        def sb(name, shape, dtype, tag=None):
+            return keep.tile(shape, dtype, name=name, tag=tag or name, align_bytes=64)
 
         offsets = keep.tile([P, S // LIST_ROWS], U16, name="offsets")
-        nc.sync.dma_start(offsets[:], offs)
 
         w4_codes = sb("w4_codes", [P, 2 * N], U8)
         w4_scale = sb("w4_scale", [P, N], U8)
-        nc.gpsimd.memset(w4_scale[:], 0)
-        nc.gpsimd.dma_start(w4_codes[:].bitcast(I32), w4_words[0].bitcast(I32))
+        nc.vector.memset(w4_scale[:].bitcast(I32), 0)
+        nc.scalar.dma_start(w4_codes[:].bitcast(I32), w4_words[0].bitcast(I32))
         for q in range(4):
-            nc.gpsimd.dma_start(w4_scale[32 * q : 32 * q + 4, :].bitcast(I32), w4_scales[0, 4 * q : 4 * q + 4, :].bitcast(I32))
+            nc.scalar.dma_start(w4_scale[32 * q : 32 * q + 4, :].bitcast(I32), w4_scales[0, 4 * q : 4 * q + 4, :].bitcast(I32))
 
         x_plane = {}
         for g in range(PASSES):
@@ -54,12 +53,14 @@ def tile_picked_trilin_relu_e_kernel(tc, xT, w1, w2, w3, w4_words, w4_scales, of
             for j in range(PACK):
                 x_plane[g, j] = sb("x_plane%d%d" % (g, j), [P, T], F32)
                 nc.sync.dma_start(x_plane[g, j][:], rows[:, j, :])
+                if (g, j) == (0, 0):
+                    nc.sync.dma_start(offsets[:], offs)
         w_raw = {}
         for d in range(PIECES):
             for g in range(PASSES):
                 rows = weights[d][g * K_PASS : (g + 1) * K_PASS, :].rearrange("(p j) c -> p j c", j=PACK)
                 last = d == PIECES - 1 and g == PASSES - 1
-                cuts = [0, 256, H] if last else [0, H]
+                cuts = [0, H] if last else [0, H]
                 w_raw[d, g] = []
                 for a, b in zip(cuts, cuts[1:]):
                     raw = sb("w_raw%d%d_%d" % (d, g, a), [P, PACK, b - a], F32)
@@ -74,7 +75,8 @@ def tile_picked_trilin_relu_e_kernel(tc, xT, w1, w2, w3, w4_words, w4_scales, of
                 x_woven[d, g] = sb("x_woven%d%d" % (d, g), [P, V, PACK], BF16)
                 x_codes[d, g] = sb("x_codes%d%d" % (d, g), [P, V], U32)
                 x_scale[d, g] = sb("x_scale%d%d" % (d, g), [P, V], U8)
-                w_woven[d, g] = sb("w_woven%d%d" % (d, g), [P, PACK, P, PACK], BF16)
+                for u in range(2):
+                    w_woven[d, g, u] = sb("w_woven%d%d%d" % (d, g, u), [P, 2, P, PACK], BF16)
                 w_codes[d, g] = sb("w_codes%d%d" % (d, g), [P, H], U32)
                 w_scale[d, g] = sb("w_scale%d%d" % (d, g), [P, H], U8)
 
@@ -94,19 +96,19 @@ def tile_picked_trilin_relu_e_kernel(tc, xT, w1, w2, w3, w4_words, w4_scales, of
                 in_=x_woven[d, g][:].rearrange("p v j -> p (v j)"),
             )
 
-        def weave_w(copy, d, g, a, b):
-            for lo, hi, raw in w_raw[d, g]:
-                if lo <= a and b <= hi:
-                    copy(
-                        w_woven[d, g][:, :, a // PACK : b // PACK, :].rearrange("p t m j -> p m j t"),
-                        raw[:, :, a - lo : b - lo].rearrange("p j (m t) -> p m j t", t=PACK),
-                    )
+        def weave_w(copy, d, g, u, chunk=0):
+            lo, hi, raw = w_raw[d, g][chunk]
+            copy(
+                w_woven[d, g, u][:, :, lo // PACK : hi // PACK, :].rearrange("p t m j -> p m j t"),
+                raw[:].rearrange("p j (m t) -> p m j t", t=PACK)[:, :, :, 2 * u : 2 * u + 2],
+            )
 
         def quantize_w(d, g, t0, t1):
+            u = t0 // 2
             nc.vector.quantize_mx(
                 out=w_codes[d, g][:, t0 * P : t1 * P].bitcast(FP8X4),
                 scales=w_scale[d, g][:, t0 * P : t1 * P],
-                in_=w_woven[d, g][:, t0:t1, :, :].rearrange("p t m j -> p (t m j)"),
+                in_=w_woven[d, g, u][:, t0 - 2 * u : t1 - 2 * u, :, :].rearrange("p t m j -> p (t m j)"),
             )
 
         y = {(d, h): psum.tile([P, PACK, HALF], F32, name="y%d%d" % (d, h)) for d in range(PIECES) for h in range(2)}
@@ -130,13 +132,11 @@ def tile_picked_trilin_relu_e_kernel(tc, xT, w1, w2, w3, w4_words, w4_scales, of
             return y[d, h][:].rearrange("p t v -> p v t")
 
         on_vector, on_scalar = nc.vector.tensor_copy, nc.scalar.copy
-        y1 = [sb("y1_%d" % h, [P, HALF, PACK], F32) for h in range(2)]
-        y12 = [sb("y12_%d" % h, [P, HALF, PACK], F32) for h in range(2)]
+        y12 = {}
         z = [sb("z%d" % h, [P, HALF, PACK], BF16) for h in range(2)]
         z_codes = [sb("z_codes%d" % h, [P, HALF], U32) for h in range(2)]
         z_scale = [sb("z_scale%d" % h, [P, HALF], U8) for h in range(2)]
         res = [sb("res%d" % h, [P, HALF], F32) for h in range(2)]
-        acc = [psum.tile([P, HALF], F32, name="acc%d" % h) for h in range(2)]
 
         for j in range(PACK):
             gather(0, j, 0, S)
@@ -148,36 +148,45 @@ def tile_picked_trilin_relu_e_kernel(tc, xT, w1, w2, w3, w4_words, w4_scales, of
         for d in range(PIECES):
             gather(1, PACK - 1, d * V, (d + 1) * V)
             weave_x(d, 1)
-        weave_w(on_vector, 0, 0, 0, H)
+        weave_w(on_vector, 0, 0, 0)
+        weave_w(on_vector, 0, 0, 1)
         quantize_x(0, 1)
-        quantize_w(0, 0, 0, PACK)
-        weave_w(on_vector, 0, 1, 0, H)
+        quantize_w(0, 0, 0, 2)
+        quantize_w(0, 0, 2, 4)
+        weave_w(on_vector, 0, 1, 0)
+        weave_w(on_scalar, 0, 1, 1)
         quantize_x(1, 1)
+        quantize_w(0, 1, 0, 2)
         quantize_x(2, 1)
-        quantize_w(0, 1, 0, PACK)
+        quantize_w(0, 1, 2, 4)
         product(0, 0)
         product(0, 1)
-        weave_w(on_scalar, 1, 0, 0, 256)
-        weave_w(on_vector, 1, 0, 256, H)
-        quantize_w(1, 0, 0, PACK)
+        weave_w(on_vector, 1, 0, 0)
+        weave_w(on_scalar, 1, 0, 1)
+        quantize_w(1, 0, 0, 2)
+        quantize_w(1, 0, 2, 4)
+        weave_w(on_vector, 1, 1, 0)
+        weave_w(on_scalar, 1, 1, 1)
+        y1 = sb("y1", [P, 2, HALF, PACK], F32, "w_raw10_0")
         for h in range(2):
-            nc.scalar.copy(y1[h][:], by_triple(0, h))
-        weave_w(on_scalar, 1, 1, 0, 128)
-        weave_w(on_vector, 1, 1, 128, H)
+            nc.scalar.copy(y1[:, h], by_triple(0, h))
         quantize_w(1, 1, 0, 2)
         quantize_w(1, 1, 2, 4)
         product(1, 0)
         product(1, 1)
-        weave_w(on_scalar, 2, 0, 0, 256)
-        weave_w(on_vector, 2, 0, 256, H)
-        nc.vector.tensor_tensor(y12[0][:], by_triple(1, 0), y1[0][:], MULT)
-        quantize_w(2, 0, 0, PACK)
-        nc.vector.tensor_tensor(y12[1][:], by_triple(1, 1), y1[1][:], MULT)
-        weave_w(on_scalar, 2, 1, 0, 256)
-        weave_w(on_scalar, 2, 1, 256, 320)
-        weave_w(on_vector, 2, 1, 320, H)
+        weave_w(on_vector, 2, 0, 0)
+        weave_w(on_scalar, 2, 0, 1)
+        y12[0] = sb("y12_0", [P, HALF, PACK], F32, "w_raw20_0")
+        nc.vector.tensor_tensor(y12[0][:], by_triple(1, 0), y1[:, 0], MULT)
+        quantize_w(2, 0, 0, 2)
+        weave_w(on_vector, 2, 1, 0)
+        weave_w(on_scalar, 2, 1, 1)
+        quantize_w(2, 0, 2, 4)
         for t in range(PACK):
             quantize_w(2, 1, t, t + 1)
+        y12[1] = sb("y12_1", [P, HALF, PACK], F32, "w_raw21_0")
+        nc.vector.tensor_tensor(y12[1][:], by_triple(1, 1), y1[:, 1], MULT)
+        acc = [psum.tile([P, HALF], F32, name="acc%d" % h) for h in range(2)]
         product(2, 0)
         product(2, 1)
         for h in range(2):

@@ -23,8 +23,12 @@ K_PASS = P * PACK
 PASSES = K // K_PASS
 S = PIECES * V
 HALF = V // 2
+PAIR = PACK // 2
 LIST_ROWS = 16
 RUN = 4
+QUADRANT = 32
+SCALE_ROWS = 4
+WARM_PASSES = 6
 
 
 def tile_picked_trilin_relu_e_kernel(tc, xT, w1, w2, w3, w4_words, w4_scales, offs, out):
@@ -35,23 +39,26 @@ def tile_picked_trilin_relu_e_kernel(tc, xT, w1, w2, w3, w4_words, w4_scales, of
         keep = ctx.enter_context(tc.tile_pool(name="keep", bufs=1))
         psum = ctx.enter_context(tc.psum_pool(name="psum", bufs=1))
 
-        def sb(name, shape, dtype, tag=None):
-            return keep.tile(shape, dtype, name=name, tag=tag or name, align_bytes=64)
+        def sbuf(name, shape, dtype, over=None):
+            return keep.tile(shape, dtype, name=name, tag=over or name, align_bytes=64)
 
         offsets = keep.tile([P, S // LIST_ROWS], U16, name="offsets")
 
-        w4_codes = sb("w4_codes", [P, 2 * N], U8)
-        w4_scale = sb("w4_scale", [P, N], U8)
+        w4_codes = sbuf("w4_codes", [P, 2 * N], U8)
+        w4_scale = sbuf("w4_scale", [P, N], U8)
         nc.vector.memset(w4_scale[:].bitcast(I32), 0)
         nc.scalar.dma_start(w4_codes[:].bitcast(I32), w4_words[0].bitcast(I32))
-        for q in range(4):
-            nc.scalar.dma_start(w4_scale[32 * q : 32 * q + 4, :].bitcast(I32), w4_scales[0, 4 * q : 4 * q + 4, :].bitcast(I32))
+        for q in range(P // QUADRANT):
+            nc.scalar.dma_start(
+                w4_scale[QUADRANT * q : QUADRANT * q + SCALE_ROWS, :].bitcast(I32),
+                w4_scales[0, SCALE_ROWS * q : SCALE_ROWS * (q + 1), :].bitcast(I32),
+            )
 
         x_plane = {}
         for g in range(PASSES):
             rows = xT[g * K_PASS : (g + 1) * K_PASS, :].rearrange("(p j) c -> p j c", j=PACK)
             for j in range(PACK):
-                x_plane[g, j] = sb("x_plane%d%d" % (g, j), [P, T], F32)
+                x_plane[g, j] = sbuf("x_plane%d%d" % (g, j), [P, T], F32)
                 nc.sync.dma_start(x_plane[g, j][:], rows[:, j, :])
                 if (g, j) == (0, 0):
                     nc.sync.dma_start(offsets[:], offs)
@@ -59,34 +66,30 @@ def tile_picked_trilin_relu_e_kernel(tc, xT, w1, w2, w3, w4_words, w4_scales, of
         for d in range(PIECES):
             for g in range(PASSES):
                 rows = weights[d][g * K_PASS : (g + 1) * K_PASS, :].rearrange("(p j) c -> p j c", j=PACK)
-                last = d == PIECES - 1 and g == PASSES - 1
-                cuts = [0, H] if last else [0, H]
-                w_raw[d, g] = []
-                for a, b in zip(cuts, cuts[1:]):
-                    raw = sb("w_raw%d%d_%d" % (d, g, a), [P, PACK, b - a], F32)
-                    nc.sync.dma_start(raw[:], rows[:, :, a:b])
-                    w_raw[d, g].append((a, b, raw))
+                w_raw[d, g] = sbuf("w_raw%d%d_0" % (d, g), [P, PACK, H], F32)
+                nc.sync.dma_start(w_raw[d, g][:], rows)
 
-        picked = {g: sb("picked%d" % g, [P, PACK, S], BF16) for g in range(PASSES)}
+        picked = {g: sbuf("picked%d" % g, [P, PACK, S], BF16) for g in range(PASSES)}
         x_woven, x_codes, x_scale = {}, {}, {}
         w_woven, w_codes, w_scale = {}, {}, {}
         for d in range(PIECES):
             for g in range(PASSES):
-                x_woven[d, g] = sb("x_woven%d%d" % (d, g), [P, V, PACK], BF16)
-                x_codes[d, g] = sb("x_codes%d%d" % (d, g), [P, V], U32)
-                x_scale[d, g] = sb("x_scale%d%d" % (d, g), [P, V], U8)
-                for u in range(2):
-                    w_woven[d, g, u] = sb("w_woven%d%d%d" % (d, g, u), [P, 2, P, PACK], BF16)
-                w_codes[d, g] = sb("w_codes%d%d" % (d, g), [P, H], U32)
-                w_scale[d, g] = sb("w_scale%d%d" % (d, g), [P, H], U8)
+                x_woven[d, g] = sbuf("x_woven%d%d" % (d, g), [P, V, PACK], BF16)
+                x_codes[d, g] = sbuf("x_codes%d%d" % (d, g), [P, V], U32)
+                x_scale[d, g] = sbuf("x_scale%d%d" % (d, g), [P, V], U8)
+                for u in range(PACK // PAIR):
+                    w_woven[d, g, u] = sbuf("w_woven%d%d%d" % (d, g, u), [P, PAIR, P, PACK], BF16)
+                w_codes[d, g] = sbuf("w_codes%d%d" % (d, g), [P, H], U32)
+                w_scale[d, g] = sbuf("w_scale%d%d" % (d, g), [P, H], U8)
 
-        def gather(g, j, a, b):
-            nc.vector.tensor_copy(picked[g][:, j, a:b], x_plane[g, j][:].indirect(offsets[:, a // LIST_ROWS : b // LIST_ROWS]))
+        def gather(g, j, first, end):
+            entries = offsets[:, first // LIST_ROWS : end // LIST_ROWS]
+            nc.vector.tensor_copy(picked[g][:, j, first:end], x_plane[g, j][:].indirect(entries))
 
         def weave_x(d, g):
             nc.scalar.copy(
-                x_woven[d, g][:].rearrange("p (c i) j -> p c j i", i=RUN),
-                picked[g][:, :, d * V : (d + 1) * V].rearrange("p j (c i) -> p c j i", i=RUN),
+                x_woven[d, g][:].rearrange("p (c r) j -> p c j r", r=RUN),
+                picked[g][:, :, d * V : (d + 1) * V].rearrange("p j (c r) -> p c j r", r=RUN),
             )
 
         def quantize_x(d, g):
@@ -96,47 +99,46 @@ def tile_picked_trilin_relu_e_kernel(tc, xT, w1, w2, w3, w4_words, w4_scales, of
                 in_=x_woven[d, g][:].rearrange("p v j -> p (v j)"),
             )
 
-        def weave_w(copy, d, g, u, chunk=0):
-            lo, hi, raw = w_raw[d, g][chunk]
+        def weave_w(copy, d, g, u):
             copy(
-                w_woven[d, g, u][:, :, lo // PACK : hi // PACK, :].rearrange("p t m j -> p m j t"),
-                raw[:].rearrange("p j (m t) -> p m j t", t=PACK)[:, :, :, 2 * u : 2 * u + 2],
+                w_woven[d, g, u][:].rearrange("p t m j -> p m j t"),
+                w_raw[d, g][:].rearrange("p j (m t) -> p m j t", t=PACK)[:, :, :, PAIR * u : PAIR * (u + 1)],
             )
 
-        def quantize_w(d, g, t0, t1):
-            u = t0 // 2
+        def quantize_w(d, g, first, end):
+            u = first // PAIR
             nc.vector.quantize_mx(
-                out=w_codes[d, g][:, t0 * P : t1 * P].bitcast(FP8X4),
-                scales=w_scale[d, g][:, t0 * P : t1 * P],
-                in_=w_woven[d, g, u][:, t0 - 2 * u : t1 - 2 * u, :, :].rearrange("p t m j -> p (t m j)"),
+                out=w_codes[d, g][:, first * P : end * P].bitcast(FP8X4),
+                scales=w_scale[d, g][:, first * P : end * P],
+                in_=w_woven[d, g, u][:, first - PAIR * u : end - PAIR * u, :, :].rearrange("p t m j -> p (t m j)"),
             )
 
         y = {(d, h): psum.tile([P, PACK, HALF], F32, name="y%d%d" % (d, h)) for d in range(PIECES) for h in range(2)}
 
-        def product(d, h):
-            cols = slice(h * HALF, (h + 1) * HALF)
-            for t in range(PACK):
-                chans = slice(t * P, (t + 1) * P)
-                for g in range(PASSES):
-                    nc.tensor.matmul_mx(
-                        out=y[d, h][:, t, :],
-                        lhsT=w_codes[d, g][:, chans].bitcast(FP8X4),
-                        lhsT_scale=w_scale[d, g][:, chans],
-                        rhs=x_codes[d, g][:, cols].bitcast(FP8X4),
-                        rhs_scale=x_scale[d, g][:, cols],
-                        start=(g == 0),
-                        stop=(g == PASSES - 1),
-                    )
+        def product(d):
+            for h in range(2):
+                triples = slice(h * HALF, (h + 1) * HALF)
+                for t in range(PACK):
+                    columns = slice(t * P, (t + 1) * P)
+                    for g in range(PASSES):
+                        nc.tensor.matmul_mx(
+                            out=y[d, h][:, t, :],
+                            lhsT=w_codes[d, g][:, columns].bitcast(FP8X4),
+                            lhsT_scale=w_scale[d, g][:, columns],
+                            rhs=x_codes[d, g][:, triples].bitcast(FP8X4),
+                            rhs_scale=x_scale[d, g][:, triples],
+                            start=(g == 0),
+                            stop=(g == PASSES - 1),
+                        )
 
         def by_triple(d, h):
             return y[d, h][:].rearrange("p t v -> p v t")
 
         on_vector, on_scalar = nc.vector.tensor_copy, nc.scalar.copy
-        y12 = {}
-        z = [sb("z%d" % h, [P, HALF, PACK], BF16) for h in range(2)]
-        z_codes = [sb("z_codes%d" % h, [P, HALF], U32) for h in range(2)]
-        z_scale = [sb("z_scale%d" % h, [P, HALF], U8) for h in range(2)]
-        res = [sb("res%d" % h, [P, HALF], F32) for h in range(2)]
+        z = [sbuf("z%d" % h, [P, HALF, PACK], BF16) for h in range(2)]
+        z_codes = [sbuf("z_codes%d" % h, [P, HALF], U32) for h in range(2)]
+        z_scale = [sbuf("z_scale%d" % h, [P, HALF], U8) for h in range(2)]
+        res = [sbuf("res%d" % h, [P, HALF], F32) for h in range(2)]
 
         for j in range(PACK):
             gather(0, j, 0, S)
@@ -148,51 +150,73 @@ def tile_picked_trilin_relu_e_kernel(tc, xT, w1, w2, w3, w4_words, w4_scales, of
         for d in range(PIECES):
             gather(1, PACK - 1, d * V, (d + 1) * V)
             weave_x(d, 1)
+
         weave_w(on_vector, 0, 0, 0)
         weave_w(on_vector, 0, 0, 1)
         quantize_x(0, 1)
-        quantize_w(0, 0, 0, 2)
-        quantize_w(0, 0, 2, 4)
+        quantize_w(0, 0, 0, PAIR)
+        quantize_w(0, 0, PAIR, PACK)
         weave_w(on_vector, 0, 1, 0)
         weave_w(on_scalar, 0, 1, 1)
         quantize_x(1, 1)
-        quantize_w(0, 1, 0, 2)
+        quantize_w(0, 1, 0, PAIR)
         quantize_x(2, 1)
-        quantize_w(0, 1, 2, 4)
-        product(0, 0)
-        product(0, 1)
+        quantize_w(0, 1, PAIR, PACK)
+        product(0)
+
         weave_w(on_vector, 1, 0, 0)
         weave_w(on_scalar, 1, 0, 1)
-        quantize_w(1, 0, 0, 2)
-        quantize_w(1, 0, 2, 4)
+        quantize_w(1, 0, 0, PAIR)
+        quantize_w(1, 0, PAIR, PACK)
         weave_w(on_vector, 1, 1, 0)
         weave_w(on_scalar, 1, 1, 1)
-        y1 = sb("y1", [P, 2, HALF, PACK], F32, "w_raw10_0")
+        y1 = sbuf("y1", [P, 2, HALF, PACK], F32, over="w_raw%d%d_0" % (1, 0))
         for h in range(2):
             nc.scalar.copy(y1[:, h], by_triple(0, h))
-        quantize_w(1, 1, 0, 2)
-        quantize_w(1, 1, 2, 4)
-        product(1, 0)
-        product(1, 1)
+        quantize_w(1, 1, 0, PAIR)
+        quantize_w(1, 1, PAIR, PACK)
+        product(1)
+
+        def multiply_y1_y2(h):
+            y12_half = sbuf("y12_%d" % h, [P, HALF, PACK], F32, over="w_raw%d%d_0" % (2, h))
+            nc.vector.tensor_tensor(y12_half[:], by_triple(1, h), y1[:, h], MULT)
+            return y12_half
+
         weave_w(on_vector, 2, 0, 0)
         weave_w(on_scalar, 2, 0, 1)
-        y12[0] = sb("y12_0", [P, HALF, PACK], F32, "w_raw20_0")
-        nc.vector.tensor_tensor(y12[0][:], by_triple(1, 0), y1[:, 0], MULT)
-        quantize_w(2, 0, 0, 2)
+        y12 = [multiply_y1_y2(0)]
+        quantize_w(2, 0, 0, PAIR)
+
+        warm = psum.tile([P, V], F32, name="acc0")
+        for n in range(WARM_PASSES):
+            columns = slice(n % PAIR * P, (n % PAIR + 1) * P)
+            nc.tensor.matmul_mx(
+                out=warm[:],
+                lhsT=w_codes[2, 0][:, columns].bitcast(FP8X4),
+                lhsT_scale=w_scale[2, 0][:, columns],
+                rhs=x_codes[2, 0][:].bitcast(FP8X4),
+                rhs_scale=x_scale[2, 0][:],
+                start=True,
+                stop=True,
+            )
+
         weave_w(on_vector, 2, 1, 0)
         weave_w(on_scalar, 2, 1, 1)
-        quantize_w(2, 0, 2, 4)
+        quantize_w(2, 0, PAIR, PACK)
         for t in range(PACK):
             quantize_w(2, 1, t, t + 1)
-        y12[1] = sb("y12_1", [P, HALF, PACK], F32, "w_raw21_0")
-        nc.vector.tensor_tensor(y12[1][:], by_triple(1, 1), y1[:, 1], MULT)
+        y12.append(multiply_y1_y2(1))
         acc = [psum.tile([P, HALF], F32, name="acc%d" % h) for h in range(2)]
-        product(2, 0)
-        product(2, 1)
+        product(2)
+
         for h in range(2):
             nc.vector.tensor_tensor(z[h][:], by_triple(2, h), y12[h][:], MULT)
         for h in range(2):
-            nc.vector.quantize_mx(out=z_codes[h][:].bitcast(FP8X4), scales=z_scale[h][:], in_=z[h][:].rearrange("p v t -> p (v t)"))
+            nc.vector.quantize_mx(
+                out=z_codes[h][:].bitcast(FP8X4),
+                scales=z_scale[h][:],
+                in_=z[h][:].rearrange("p v t -> p (v t)"),
+            )
             nc.tensor.matmul_mx(
                 out=acc[h][:],
                 lhsT=w4_codes[:].bitcast(FP4X4),
@@ -202,6 +226,7 @@ def tile_picked_trilin_relu_e_kernel(tc, xT, w1, w2, w3, w4_words, w4_scales, of
                 start=True,
                 stop=True,
             )
+
         nc.scalar.activation(res[0][:], acc[0][:], RELU)
         nc.scalar.dma_start(out[:, 0:HALF], res[0][:])
         nc.vector.tensor_scalar_max(res[1][:], acc[1][:], 0.0)

@@ -28,7 +28,6 @@ LIST_ROWS = 16
 RUN = 4
 QUADRANT = 32
 SCALE_ROWS = 4
-WARM_PASSES = 6
 
 
 def tile_picked_trilin_relu_e_kernel(tc, xT, w1, w2, w3, w4_words, w4_scales, offs, out):
@@ -99,10 +98,10 @@ def tile_picked_trilin_relu_e_kernel(tc, xT, w1, w2, w3, w4_words, w4_scales, of
                 in_=x_woven[d, g][:].rearrange("p v j -> p (v j)"),
             )
 
-        def weave_w(copy, d, g, u):
+        def weave_w(copy, d, g, u, first=0, end=P):
             copy(
-                w_woven[d, g, u][:].rearrange("p t m j -> p m j t"),
-                w_raw[d, g][:].rearrange("p j (m t) -> p m j t", t=PACK)[:, :, :, PAIR * u : PAIR * (u + 1)],
+                w_woven[d, g, u][:, :, first:end].rearrange("p t m j -> p m j t"),
+                w_raw[d, g][:].rearrange("p j (m t) -> p m j t", t=PACK)[:, first:end, :, PAIR * u : PAIR * (u + 1)],
             )
 
         def quantize_w(d, g, first, end):
@@ -113,23 +112,38 @@ def tile_picked_trilin_relu_e_kernel(tc, xT, w1, w2, w3, w4_words, w4_scales, of
                 in_=w_woven[d, g, u][:, first - PAIR * u : end - PAIR * u, :, :].rearrange("p t m j -> p (t m j)"),
             )
 
+        def warm_up(d, g, count, width):
+            for n in range(count):
+                nc.tensor.matmul_mx(
+                    out=warm[:, 0:width],
+                    lhsT=w_codes[d, g][:, 0:P].bitcast(FP8X4),
+                    lhsT_scale=w_scale[d, g][:, 0:P],
+                    rhs=w_codes[d, g][:, 0:width].bitcast(FP8X4),
+                    rhs_scale=w_scale[d, g][:, 0:width],
+                    start=True,
+                    stop=True,
+                )
+
         y = {(d, h): psum.tile([P, PACK, HALF], F32, name="y%d%d" % (d, h)) for d in range(PIECES) for h in range(2)}
 
+        def product_pass(d, g):
+            for t in range(PACK):
+                columns = slice(t * P, (t + 1) * P)
+                for h in range(2):
+                    triples = slice(h * HALF, (h + 1) * HALF)
+                    nc.tensor.matmul_mx(
+                        out=y[d, h][:, t, :],
+                        lhsT=w_codes[d, g][:, columns].bitcast(FP8X4),
+                        lhsT_scale=w_scale[d, g][:, columns],
+                        rhs=x_codes[d, g][:, triples].bitcast(FP8X4),
+                        rhs_scale=x_scale[d, g][:, triples],
+                        start=(g == 0 and t == 0),
+                        stop=(g == PASSES - 1 and t == PACK - 1),
+                    )
+
         def product(d):
-            for h in range(2):
-                triples = slice(h * HALF, (h + 1) * HALF)
-                for t in range(PACK):
-                    columns = slice(t * P, (t + 1) * P)
-                    for g in range(PASSES):
-                        nc.tensor.matmul_mx(
-                            out=y[d, h][:, t, :],
-                            lhsT=w_codes[d, g][:, columns].bitcast(FP8X4),
-                            lhsT_scale=w_scale[d, g][:, columns],
-                            rhs=x_codes[d, g][:, triples].bitcast(FP8X4),
-                            rhs_scale=x_scale[d, g][:, triples],
-                            start=(g == 0),
-                            stop=(g == PASSES - 1),
-                        )
+            for g in range(PASSES):
+                product_pass(d, g)
 
         def by_triple(d, h):
             return y[d, h][:].rearrange("p t v -> p v t")
@@ -168,46 +182,34 @@ def tile_picked_trilin_relu_e_kernel(tc, xT, w1, w2, w3, w4_words, w4_scales, of
         weave_w(on_scalar, 1, 0, 1)
         quantize_w(1, 0, 0, PAIR)
         quantize_w(1, 0, PAIR, PACK)
+        y1 = [sbuf("y1_%d" % h, [P, HALF, PACK], F32, over="w_raw1%d_0" % h) for h in range(2)]
+        nc.scalar.copy(y1[0][:], by_triple(0, 0))
         weave_w(on_vector, 1, 1, 0)
-        weave_w(on_scalar, 1, 1, 1)
-        y1 = sbuf("y1", [P, 2, HALF, PACK], F32, over="w_raw%d%d_0" % (1, 0))
-        for h in range(2):
-            nc.scalar.copy(y1[:, h], by_triple(0, h))
-        quantize_w(1, 1, 0, PAIR)
-        quantize_w(1, 1, PAIR, PACK)
+        weave_w(on_vector, 1, 1, 1, 0, P // 2)
+        weave_w(on_scalar, 1, 1, 1, P // 2, P)
+        nc.scalar.copy(y1[1][:], by_triple(0, 1))
+        for t in range(PACK):
+            quantize_w(1, 1, t, t + 1)
         product(1)
 
-        def multiply_y1_y2(h):
-            y12_half = sbuf("y12_%d" % h, [P, HALF, PACK], F32, over="w_raw%d%d_0" % (2, h))
-            nc.vector.tensor_tensor(y12_half[:], by_triple(1, h), y1[:, h], MULT)
-            return y12_half
-
-        weave_w(on_vector, 2, 0, 0)
+        y12 = [sbuf("y12_%d" % h, [P, HALF, PACK], F32) for h in range(2)]
+        nc.vector.tensor_tensor(y12[0][:], by_triple(1, 0), y1[0][:], MULT)
+        warm = psum.tile([P, H], F32, name="y10")
+        warm_up(1, 1, 2, H)
+        weave_w(on_vector, 2, 0, 0, 0, P // 2)
         weave_w(on_scalar, 2, 0, 1)
-        y12 = [multiply_y1_y2(0)]
-        quantize_w(2, 0, 0, PAIR)
-
-        warm = psum.tile([P, V], F32, name="acc0")
-        for n in range(WARM_PASSES):
-            columns = slice(n % PAIR * P, (n % PAIR + 1) * P)
-            nc.tensor.matmul_mx(
-                out=warm[:],
-                lhsT=w_codes[2, 0][:, columns].bitcast(FP8X4),
-                lhsT_scale=w_scale[2, 0][:, columns],
-                rhs=x_codes[2, 0][:].bitcast(FP8X4),
-                rhs_scale=x_scale[2, 0][:],
-                start=True,
-                stop=True,
-            )
-
-        weave_w(on_vector, 2, 1, 0)
-        weave_w(on_scalar, 2, 1, 1)
+        weave_w(on_scalar, 2, 0, 0, P // 2, P)
+        nc.vector.tensor_tensor(y12[1][:], by_triple(1, 1), y1[1][:], MULT)
         quantize_w(2, 0, PAIR, PACK)
+        quantize_w(2, 0, 0, PAIR)
+        weave_w(on_vector, 2, 1, 0)
+        weave_w(on_scalar, 2, 1, 1, P // 4, P)
+        weave_w(on_vector, 2, 1, 1, 0, P // 4)
         for t in range(PACK):
             quantize_w(2, 1, t, t + 1)
-        y12.append(multiply_y1_y2(1))
         acc = [psum.tile([P, HALF], F32, name="acc%d" % h) for h in range(2)]
         product(2)
+        warm_up(2, 1, 1, H)
 
         for h in range(2):
             nc.vector.tensor_tensor(z[h][:], by_triple(2, h), y12[h][:], MULT)

@@ -26,6 +26,7 @@ HALF = V // 2
 PAIR = PACK // 2
 LIST_ROWS = 16
 RUN = 4
+EARLY = 64
 QUADRANT = 32
 SCALE_ROWS = 4
 
@@ -185,9 +186,9 @@ def tile_picked_trilin_relu_e_kernel(tc, xT, w1, w2, w3, w4_words, w4_scales, of
         y1 = [sbuf("y1_%d" % h, [P, HALF, PACK], F32, over="w_raw1%d_0" % h) for h in range(2)]
         nc.scalar.copy(y1[0][:], by_triple(0, 0))
         weave_w(on_vector, 1, 1, 0)
-        weave_w(on_vector, 1, 1, 1, 0, P // 2)
-        weave_w(on_scalar, 1, 1, 1, P // 2, P)
-        nc.scalar.copy(y1[1][:], by_triple(0, 1))
+        weave_w(on_vector, 1, 1, 1, 0, P // 4)
+        weave_w(on_scalar, 1, 1, 1, P // 4, P)
+        nc.scalar.copy(y1[1][:, :EARLY], by_triple(0, 1)[:, :EARLY])
         for t in range(PACK):
             quantize_w(1, 1, t, t + 1)
         product(1)
@@ -196,10 +197,10 @@ def tile_picked_trilin_relu_e_kernel(tc, xT, w1, w2, w3, w4_words, w4_scales, of
         nc.vector.tensor_tensor(y12[0][:], by_triple(1, 0), y1[0][:], MULT)
         warm = psum.tile([P, H], F32, name="y10")
         warm_up(1, 1, 2, H)
-        weave_w(on_vector, 2, 0, 0, 0, P // 2)
+        weave_w(on_vector, 2, 0, 0, 0, 3 * P // 4)
         weave_w(on_scalar, 2, 0, 1)
-        weave_w(on_scalar, 2, 0, 0, P // 2, P)
-        nc.vector.tensor_tensor(y12[1][:], by_triple(1, 1), y1[1][:], MULT)
+        weave_w(on_scalar, 2, 0, 0, 3 * P // 4, P)
+        nc.vector.tensor_tensor(y12[1][:, :EARLY], by_triple(1, 1)[:, :EARLY], y1[1][:, :EARLY], MULT)
         quantize_w(2, 0, PAIR, PACK)
         quantize_w(2, 0, 0, PAIR)
         weave_w(on_vector, 2, 1, 0)
@@ -207,6 +208,9 @@ def tile_picked_trilin_relu_e_kernel(tc, xT, w1, w2, w3, w4_words, w4_scales, of
         weave_w(on_vector, 2, 1, 1, 0, P // 4)
         for t in range(PACK):
             quantize_w(2, 1, t, t + 1)
+        y1_late = sbuf("y1_late", [P, HALF - EARLY, PACK], F32, over="w_raw21_0")
+        nc.scalar.copy(y1_late[:], by_triple(0, 1)[:, EARLY:])
+        nc.vector.tensor_tensor(y12[1][:, EARLY:], by_triple(1, 1)[:, EARLY:], y1_late[:], MULT)
         acc = [psum.tile([P, HALF], F32, name="acc%d" % h) for h in range(2)]
         product(2)
         warm_up(2, 1, 1, H)

@@ -40,7 +40,7 @@ def tile_picked_trilin_relu_e_kernel(tc, xT, w1, w2, w3, w4_words, w4_scales, of
         psum = ctx.enter_context(tc.psum_pool(name="psum", bufs=1))
 
         def sbuf(name, shape, dtype, over=None):
-            return keep.tile(shape, dtype, name=name, tag=over or name, align_bytes=64)
+            return keep.tile(shape, dtype, name=name, tag=over or name, align_bytes=256)
 
         offsets = keep.tile([P, S // LIST_ROWS], U16, name="offsets")
 

@@ -27,6 +27,8 @@ PAIR = PACK // 2
 LIST_ROWS = 16
 RUN = 4
 EARLY = 64
+HALVED = ((2, 0), (2, 1))
+MH = P // 2
 QUADRANT = 32
 SCALE_ROWS = 4
 
@@ -62,12 +64,17 @@ def tile_picked_trilin_relu_e_kernel(tc, xT, w1, w2, w3, w4_words, w4_scales, of
                 nc.sync.dma_start(x_plane[g, j][:], rows[:, j, :])
                 if (g, j) == (0, 0):
                     nc.sync.dma_start(offsets[:], offs)
-        w_raw = {}
+        w_raw, w_half, half_woven = {}, {}, {}
         for d in range(PIECES):
             for g in range(PASSES):
                 rows = weights[d][g * K_PASS : (g + 1) * K_PASS, :].rearrange("(p j) c -> p j c", j=PACK)
-                w_raw[d, g] = sbuf("w_raw%d%d_0" % (d, g), [P, PACK, H], F32)
-                nc.sync.dma_start(w_raw[d, g][:], rows)
+                if (d, g) in HALVED:
+                    for a in range(2):
+                        w_half[d, g, a] = sbuf("w_half%d%d%d" % (d, g, a), [P, PACK, H // 2], F32)
+                        nc.sync.dma_start(w_half[d, g, a][:], rows[:, :, a * H // 2 : (a + 1) * H // 2])
+                else:
+                    w_raw[d, g] = sbuf("w_raw%d%d_0" % (d, g), [P, PACK, H], F32)
+                    nc.sync.dma_start(w_raw[d, g][:], rows)
 
         picked = {g: sbuf("picked%d" % g, [P, PACK, S], BF16) for g in range(PASSES)}
         x_woven, x_codes, x_scale = {}, {}, {}
@@ -78,7 +85,11 @@ def tile_picked_trilin_relu_e_kernel(tc, xT, w1, w2, w3, w4_words, w4_scales, of
                 x_codes[d, g] = sbuf("x_codes%d%d" % (d, g), [P, V], U32)
                 x_scale[d, g] = sbuf("x_scale%d%d" % (d, g), [P, V], U8)
                 for u in range(PACK // PAIR):
-                    w_woven[d, g, u] = sbuf("w_woven%d%d%d" % (d, g, u), [P, PAIR, P, PACK], BF16)
+                    if (d, g) in HALVED:
+                        for a in range(2):
+                            half_woven[d, g, a, u] = sbuf("half_woven%d%d%d%d" % (d, g, a, u), [P, PAIR, MH, PACK], BF16)
+                    else:
+                        w_woven[d, g, u] = sbuf("w_woven%d%d%d" % (d, g, u), [P, PAIR, P, PACK], BF16)
                 w_codes[d, g] = sbuf("w_codes%d%d" % (d, g), [P, H], U32)
                 w_scale[d, g] = sbuf("w_scale%d%d" % (d, g), [P, H], U8)
 
@@ -113,6 +124,20 @@ def tile_picked_trilin_relu_e_kernel(tc, xT, w1, w2, w3, w4_words, w4_scales, of
                 in_=w_woven[d, g, u][:, first - PAIR * u : end - PAIR * u, :, :].rearrange("p t m j -> p (t m j)"),
             )
 
+        def weave_half(copy, d, g, a, u, first=0, end=MH):
+            copy(
+                half_woven[d, g, a, u][:, :, first:end].rearrange("p t m j -> p m j t"),
+                w_half[d, g, a][:].rearrange("p j (m t) -> p m j t", t=PACK)[:, first:end, :, PAIR * u : PAIR * (u + 1)],
+            )
+
+        def quantize_half(d, g, a, t):
+            columns = slice(t * P + a * MH, t * P + (a + 1) * MH)
+            nc.vector.quantize_mx(
+                out=w_codes[d, g][:, columns].bitcast(FP8X4),
+                scales=w_scale[d, g][:, columns],
+                in_=half_woven[d, g, a, t // PAIR][:, t % PAIR, :, :].rearrange("p m j -> p (m j)"),
+            )
+
         def warm_up(d, g, count, width):
             for n in range(count):
                 nc.tensor.matmul_mx(
@@ -128,9 +153,10 @@ def tile_picked_trilin_relu_e_kernel(tc, xT, w1, w2, w3, w4_words, w4_scales, of
         y = {(d, h): psum.tile([P, PACK, HALF], F32, name="y%d%d" % (d, h)) for d in range(PIECES) for h in range(2)}
 
         def product_pass(d, g):
-            for t in range(PACK):
-                columns = slice(t * P, (t + 1) * P)
-                for h in range(2):
+            for h in range(2):
+                order = list(range(PACK)) if h == 0 else list(reversed(range(PACK)))
+                for t in order:
+                    columns = slice(t * P, (t + 1) * P)
                     triples = slice(h * HALF, (h + 1) * HALF)
                     nc.tensor.matmul_mx(
                         out=y[d, h][:, t, :],
@@ -138,8 +164,8 @@ def tile_picked_trilin_relu_e_kernel(tc, xT, w1, w2, w3, w4_words, w4_scales, of
                         lhsT_scale=w_scale[d, g][:, columns],
                         rhs=x_codes[d, g][:, triples].bitcast(FP8X4),
                         rhs_scale=x_scale[d, g][:, triples],
-                        start=(g == 0 and t == 0),
-                        stop=(g == PASSES - 1 and t == PACK - 1),
+                        start=(g == 0 and t == order[0]),
+                        stop=(g == PASSES - 1 and t == order[-1]),
                     )
 
         def product(d):
@@ -194,21 +220,28 @@ def tile_picked_trilin_relu_e_kernel(tc, xT, w1, w2, w3, w4_words, w4_scales, of
         product(1)
 
         y12 = [sbuf("y12_%d" % h, [P, HALF, PACK], F32) for h in range(2)]
+        weave_half(on_vector, 2, 0, 0, 0)
+        weave_half(on_scalar, 2, 0, 0, 1)
         nc.vector.tensor_tensor(y12[0][:], by_triple(1, 0), y1[0][:], MULT)
         warm = psum.tile([P, H], F32, name="y10")
         warm_up(1, 1, 2, H)
-        weave_w(on_vector, 2, 0, 0, 0, 3 * P // 4)
-        weave_w(on_scalar, 2, 0, 1)
-        weave_w(on_scalar, 2, 0, 0, 3 * P // 4, P)
-        nc.vector.tensor_tensor(y12[1][:, :EARLY], by_triple(1, 1)[:, :EARLY], y1[1][:, :EARLY], MULT)
-        quantize_w(2, 0, PAIR, PACK)
-        quantize_w(2, 0, 0, PAIR)
-        weave_w(on_vector, 2, 1, 0)
-        weave_w(on_scalar, 2, 1, 1, P // 4, P)
-        weave_w(on_vector, 2, 1, 1, 0, P // 4)
         for t in range(PACK):
-            quantize_w(2, 1, t, t + 1)
-        y1_late = sbuf("y1_late", [P, HALF - EARLY, PACK], F32, over="w_raw21_0")
+            quantize_half(2, 0, 0, t)
+        weave_half(on_scalar, 2, 0, 1, 0)
+        weave_half(on_scalar, 2, 0, 1, 1)
+        nc.vector.tensor_tensor(y12[1][:, :EARLY], by_triple(1, 1)[:, :EARLY], y1[1][:, :EARLY], MULT)
+        weave_half(on_vector, 2, 1, 0, 0)
+        weave_half(on_scalar, 2, 1, 0, 1)
+        for t in range(PACK):
+            quantize_half(2, 0, 1, t)
+        for t in range(PACK):
+            quantize_half(2, 1, 0, t)
+        weave_half(on_vector, 2, 1, 1, 0)
+        weave_half(on_scalar, 2, 1, 1, 1, MH // 4, MH)
+        weave_half(on_vector, 2, 1, 1, 1, 0, MH // 4)
+        for t in range(PACK):
+            quantize_half(2, 1, 1, t)
+        y1_late = sbuf("y1_late", [P, HALF - EARLY, PACK], F32, over="w_half210")
         nc.scalar.copy(y1_late[:], by_triple(0, 1)[:, EARLY:])
         nc.vector.tensor_tensor(y12[1][:, EARLY:], by_triple(1, 1)[:, EARLY:], y1_late[:], MULT)
         acc = [psum.tile([P, HALF], F32, name="acc%d" % h) for h in range(2)]

@@ -46,16 +46,6 @@ def tile_picked_trilin_relu_e_kernel(tc, xT, w1, w2, w3, w4_words, w4_scales, of
 
         offsets = keep.tile([P, S // LIST_ROWS], U16, name="offsets")
 
-        w4_codes = sbuf("w4_codes", [P, 2 * N], U8)
-        w4_scale = sbuf("w4_scale", [P, N], U8)
-        nc.vector.memset(w4_scale[:].bitcast(I32), 0)
-        nc.scalar.dma_start(w4_codes[:].bitcast(I32), w4_words[0].bitcast(I32))
-        for q in range(P // QUADRANT):
-            nc.scalar.dma_start(
-                w4_scale[QUADRANT * q : QUADRANT * q + SCALE_ROWS, :].bitcast(I32),
-                w4_scales[0, SCALE_ROWS * q : SCALE_ROWS * (q + 1), :].bitcast(I32),
-            )
-
         x_plane = {}
         for g in range(PASSES):
             rows = xT[g * K_PASS : (g + 1) * K_PASS, :].rearrange("(p j) c -> p j c", j=PACK)
@@ -75,6 +65,16 @@ def tile_picked_trilin_relu_e_kernel(tc, xT, w1, w2, w3, w4_words, w4_scales, of
                 else:
                     w_raw[d, g] = sbuf("w_raw%d%d_0" % (d, g), [P, PACK, H], F32)
                     nc.sync.dma_start(w_raw[d, g][:], rows)
+
+        w4_codes = sbuf("w4_codes", [P, 2 * N], U8)
+        w4_scale = sbuf("w4_scale", [P, N], U8)
+        nc.vector.memset(w4_scale[:].bitcast(I32), 0)
+        nc.sync.dma_start(w4_codes[:].bitcast(I32), w4_words[0].bitcast(I32))
+        for q in range(P // QUADRANT):
+            nc.sync.dma_start(
+                w4_scale[QUADRANT * q : QUADRANT * q + SCALE_ROWS, :].bitcast(I32),
+                w4_scales[0, SCALE_ROWS * q : SCALE_ROWS * (q + 1), :].bitcast(I32),
+            )
 
         picked = {g: sbuf("picked%d" % g, [P, PACK, S], BF16) for g in range(PASSES)}
         x_woven, x_codes, x_scale = {}, {}, {}
@@ -267,6 +267,6 @@ def tile_picked_trilin_relu_e_kernel(tc, xT, w1, w2, w3, w4_words, w4_scales, of
             )
 
         nc.scalar.activation(res[0][:], acc[0][:], RELU)
-        nc.scalar.dma_start(out[:, 0:HALF], res[0][:])
+        nc.sync.dma_start(out[:, 0:HALF], res[0][:])
         nc.vector.tensor_scalar_max(res[1][:], acc[1][:], 0.0)
         nc.sync.dma_start(out[:, HALF:V], res[1][:])

@@ -4,6 +4,7 @@ import concourse.mybir as mybir
 
 K, T, V, H, N = 1024, 2048, 256, 512, 128
 PIECES = 3
+LAST = PIECES - 1
 FLOPS = 2 * PIECES * K * H * V + 2 * H * N * V
 
 F32 = mybir.dt.float32
@@ -15,7 +16,6 @@ U8 = mybir.dt.uint8
 FP8X4 = mybir.dt.float8_e4m3fn_x4
 FP4X4 = mybir.dt.float4_e2m1fn_x4
 MULT = mybir.AluOpType.mult
-RELU = mybir.ActivationFunctionType.Relu
 
 P = 128
 PACK = 4
@@ -26,9 +26,10 @@ HALF = V // 2
 PAIR = PACK // 2
 LIST_ROWS = 16
 RUN = 4
-EARLY = 64
-HALVED = ((2, 0), (2, 1))
-MH = P // 2
+SIDES = 2
+SIDE = P // SIDES
+EARLY = HALF // 2
+VECTOR_SHARE = 4
 QUADRANT = 32
 SCALE_ROWS = 4
 
@@ -54,16 +55,16 @@ def tile_picked_trilin_relu_e_kernel(tc, xT, w1, w2, w3, w4_words, w4_scales, of
                 nc.sync.dma_start(x_plane[g, j][:], rows[:, j, :])
                 if (g, j) == (0, 0):
                     nc.sync.dma_start(offsets[:], offs)
-        w_raw, w_half, half_woven = {}, {}, {}
+        w_raw, w3_raw = {}, {}
         for d in range(PIECES):
             for g in range(PASSES):
                 rows = weights[d][g * K_PASS : (g + 1) * K_PASS, :].rearrange("(p j) c -> p j c", j=PACK)
-                if (d, g) in HALVED:
-                    for a in range(2):
-                        w_half[d, g, a] = sbuf("w_half%d%d%d" % (d, g, a), [P, PACK, H // 2], F32)
-                        nc.sync.dma_start(w_half[d, g, a][:], rows[:, :, a * H // 2 : (a + 1) * H // 2])
+                if d == LAST:
+                    for a in range(SIDES):
+                        w3_raw[g, a] = sbuf("w3_raw%d%d" % (g, a), [P, PACK, H // SIDES], F32)
+                        nc.sync.dma_start(w3_raw[g, a][:], rows[:, :, a * H // SIDES : (a + 1) * H // SIDES])
                 else:
-                    w_raw[d, g] = sbuf("w_raw%d%d_0" % (d, g), [P, PACK, H], F32)
+                    w_raw[d, g] = sbuf("w_raw%d%d" % (d, g), [P, PACK, H], F32)
                     nc.sync.dma_start(w_raw[d, g][:], rows)
 
         w4_codes = sbuf("w4_codes", [P, 2 * N], U8)
@@ -78,16 +79,16 @@ def tile_picked_trilin_relu_e_kernel(tc, xT, w1, w2, w3, w4_words, w4_scales, of
 
         picked = {g: sbuf("picked%d" % g, [P, PACK, S], BF16) for g in range(PASSES)}
         x_woven, x_codes, x_scale = {}, {}, {}
-        w_woven, w_codes, w_scale = {}, {}, {}
+        w_woven, w3_woven, w_codes, w_scale = {}, {}, {}, {}
         for d in range(PIECES):
             for g in range(PASSES):
                 x_woven[d, g] = sbuf("x_woven%d%d" % (d, g), [P, V, PACK], BF16)
                 x_codes[d, g] = sbuf("x_codes%d%d" % (d, g), [P, V], U32)
                 x_scale[d, g] = sbuf("x_scale%d%d" % (d, g), [P, V], U8)
                 for u in range(PACK // PAIR):
-                    if (d, g) in HALVED:
-                        for a in range(2):
-                            half_woven[d, g, a, u] = sbuf("half_woven%d%d%d%d" % (d, g, a, u), [P, PAIR, MH, PACK], BF16)
+                    if d == LAST:
+                        for a in range(SIDES):
+                            w3_woven[g, a, u] = sbuf("w3_woven%d%d%d" % (g, a, u), [P, PAIR, SIDE, PACK], BF16)
                     else:
                         w_woven[d, g, u] = sbuf("w_woven%d%d%d" % (d, g, u), [P, PAIR, P, PACK], BF16)
                 w_codes[d, g] = sbuf("w_codes%d%d" % (d, g), [P, H], U32)
@@ -124,53 +125,50 @@ def tile_picked_trilin_relu_e_kernel(tc, xT, w1, w2, w3, w4_words, w4_scales, of
                 in_=w_woven[d, g, u][:, first - PAIR * u : end - PAIR * u, :, :].rearrange("p t m j -> p (t m j)"),
             )
 
-        def weave_half(copy, d, g, a, u, first=0, end=MH):
+        def weave_w3(copy, g, a, u, first=0, end=SIDE):
             copy(
-                half_woven[d, g, a, u][:, :, first:end].rearrange("p t m j -> p m j t"),
-                w_half[d, g, a][:].rearrange("p j (m t) -> p m j t", t=PACK)[:, first:end, :, PAIR * u : PAIR * (u + 1)],
+                w3_woven[g, a, u][:, :, first:end].rearrange("p t m j -> p m j t"),
+                w3_raw[g, a][:].rearrange("p j (m t) -> p m j t", t=PACK)[:, first:end, :, PAIR * u : PAIR * (u + 1)],
             )
 
-        def quantize_half(d, g, a, t):
-            columns = slice(t * P + a * MH, t * P + (a + 1) * MH)
-            nc.vector.quantize_mx(
-                out=w_codes[d, g][:, columns].bitcast(FP8X4),
-                scales=w_scale[d, g][:, columns],
-                in_=half_woven[d, g, a, t // PAIR][:, t % PAIR, :, :].rearrange("p m j -> p (m j)"),
-            )
-
-        def warm_up(d, g, count, width):
-            for n in range(count):
-                nc.tensor.matmul_mx(
-                    out=warm[:, 0:width],
-                    lhsT=w_codes[d, g][:, 0:P].bitcast(FP8X4),
-                    lhsT_scale=w_scale[d, g][:, 0:P],
-                    rhs=w_codes[d, g][:, 0:width].bitcast(FP8X4),
-                    rhs_scale=w_scale[d, g][:, 0:width],
-                    start=True,
-                    stop=True,
+        def quantize_w3(g, a):
+            for t in range(PACK):
+                columns = slice(t * P + a * SIDE, t * P + (a + 1) * SIDE)
+                nc.vector.quantize_mx(
+                    out=w_codes[LAST, g][:, columns].bitcast(FP8X4),
+                    scales=w_scale[LAST, g][:, columns],
+                    in_=w3_woven[g, a, t // PAIR][:, t % PAIR, :, :].rearrange("p m j -> p (m j)"),
                 )
+
+        def warm_up(d, g):
+            nc.tensor.matmul_mx(
+                out=warm[:],
+                lhsT=w_codes[d, g][:, 0:P].bitcast(FP8X4),
+                lhsT_scale=w_scale[d, g][:, 0:P],
+                rhs=w_codes[d, g][:].bitcast(FP8X4),
+                rhs_scale=w_scale[d, g][:],
+                start=True,
+                stop=True,
+            )
 
         y = {(d, h): psum.tile([P, PACK, HALF], F32, name="y%d%d" % (d, h)) for d in range(PIECES) for h in range(2)}
 
-        def product_pass(d, g):
-            for h in range(2):
-                order = list(range(PACK)) if h == 0 else list(reversed(range(PACK)))
-                for t in order:
-                    columns = slice(t * P, (t + 1) * P)
-                    triples = slice(h * HALF, (h + 1) * HALF)
-                    nc.tensor.matmul_mx(
-                        out=y[d, h][:, t, :],
-                        lhsT=w_codes[d, g][:, columns].bitcast(FP8X4),
-                        lhsT_scale=w_scale[d, g][:, columns],
-                        rhs=x_codes[d, g][:, triples].bitcast(FP8X4),
-                        rhs_scale=x_scale[d, g][:, triples],
-                        start=(g == 0 and t == order[0]),
-                        stop=(g == PASSES - 1 and t == order[-1]),
-                    )
-
         def product(d):
             for g in range(PASSES):
-                product_pass(d, g)
+                for h in range(2):
+                    order = list(range(PACK)) if h == 0 else list(reversed(range(PACK)))
+                    triples = slice(h * HALF, (h + 1) * HALF)
+                    for t in order:
+                        columns = slice(t * P, (t + 1) * P)
+                        nc.tensor.matmul_mx(
+                            out=y[d, h][:, t, :],
+                            lhsT=w_codes[d, g][:, columns].bitcast(FP8X4),
+                            lhsT_scale=w_scale[d, g][:, columns],
+                            rhs=x_codes[d, g][:, triples].bitcast(FP8X4),
+                            rhs_scale=x_scale[d, g][:, triples],
+                            start=(g == 0 and t == order[0]),
+                            stop=(g == PASSES - 1 and t == order[-1]),
+                        )
 
         def by_triple(d, h):
             return y[d, h][:].rearrange("p t v -> p v t")
@@ -185,9 +183,9 @@ def tile_picked_trilin_relu_e_kernel(tc, xT, w1, w2, w3, w4_words, w4_scales, of
             gather(0, j, 0, S)
         for d in range(PIECES):
             weave_x(d, 0)
-        for j in range(PACK - 1):
+        for j, d in zip(range(PACK - 1), range(PIECES)):
             gather(1, j, 0, S)
-            quantize_x(j, 0)
+            quantize_x(d, 0)
         for d in range(PIECES):
             gather(1, PACK - 1, d * V, (d + 1) * V)
             weave_x(d, 1)
@@ -209,53 +207,56 @@ def tile_picked_trilin_relu_e_kernel(tc, xT, w1, w2, w3, w4_words, w4_scales, of
         weave_w(on_scalar, 1, 0, 1)
         quantize_w(1, 0, 0, PAIR)
         quantize_w(1, 0, PAIR, PACK)
-        y1 = [sbuf("y1_%d" % h, [P, HALF, PACK], F32, over="w_raw1%d_0" % h) for h in range(2)]
+        y1 = [sbuf("y1_%d" % h, [P, HALF, PACK], F32, over="w_raw1%d" % h) for h in range(2)]
         nc.scalar.copy(y1[0][:], by_triple(0, 0))
         weave_w(on_vector, 1, 1, 0)
-        weave_w(on_vector, 1, 1, 1, 0, P // 4)
-        weave_w(on_scalar, 1, 1, 1, P // 4, P)
-        nc.scalar.copy(y1[1][:, :EARLY], by_triple(0, 1)[:, :EARLY])
+        weave_w(on_vector, 1, 1, 1, 0, P // VECTOR_SHARE)
+        weave_w(on_scalar, 1, 1, 1, P // VECTOR_SHARE, P)
+        nc.scalar.copy(y1[1][:], by_triple(0, 1))
         for t in range(PACK):
             quantize_w(1, 1, t, t + 1)
         product(1)
 
-        y12 = [sbuf("y12_%d" % h, [P, HALF, PACK], F32) for h in range(2)]
-        weave_half(on_vector, 2, 0, 0, 0)
-        weave_half(on_scalar, 2, 0, 0, 1)
-        nc.vector.tensor_tensor(y12[0][:], by_triple(1, 0), y1[0][:], MULT)
-        warm = psum.tile([P, H], F32, name="y10")
-        warm_up(1, 1, 2, H)
-        for t in range(PACK):
-            quantize_half(2, 0, 0, t)
-        weave_half(on_scalar, 2, 0, 1, 0)
-        weave_half(on_scalar, 2, 0, 1, 1)
-        nc.vector.tensor_tensor(y12[1][:, :EARLY], by_triple(1, 1)[:, :EARLY], y1[1][:, :EARLY], MULT)
-        weave_half(on_vector, 2, 1, 0, 0)
-        weave_half(on_scalar, 2, 1, 0, 1)
-        for t in range(PACK):
-            quantize_half(2, 0, 1, t)
-        for t in range(PACK):
-            quantize_half(2, 1, 0, t)
-        weave_half(on_vector, 2, 1, 1, 0)
-        weave_half(on_scalar, 2, 1, 1, 1, MH // 4, MH)
-        weave_half(on_vector, 2, 1, 1, 1, 0, MH // 4)
-        for t in range(PACK):
-            quantize_half(2, 1, 1, t)
-        y1_late = sbuf("y1_late", [P, HALF - EARLY, PACK], F32, over="w_half210")
-        nc.scalar.copy(y1_late[:], by_triple(0, 1)[:, EARLY:])
-        nc.vector.tensor_tensor(y12[1][:, EARLY:], by_triple(1, 1)[:, EARLY:], y1_late[:], MULT)
+        y12_first = sbuf("y12_first", [P, HALF, PACK], F32)
+        weave_w3(on_vector, 0, 0, 0)
+        weave_w3(on_scalar, 0, 0, 1)
+        nc.vector.tensor_tensor(y12_first[:], by_triple(1, 0), y1[0][:], MULT)
+        warm = psum.tile([P, H], F32, name="warm", tag="y10")
+        warm_up(1, 1)
+        warm_up(1, 1)
+        quantize_w3(0, 0)
+        weave_w3(on_scalar, 0, 1, 0)
+        weave_w3(on_scalar, 0, 1, 1)
+        y12_early = sbuf("y12_early", [P, EARLY, PACK], F32)
+        nc.vector.tensor_tensor(y12_early[:], by_triple(1, 1)[:, :EARLY], y1[1][:, :EARLY], MULT)
+        weave_w3(on_vector, 1, 0, 0)
+        weave_w3(on_scalar, 1, 0, 1)
+        quantize_w3(0, 1)
+        quantize_w3(1, 0)
+        weave_w3(on_vector, 1, 1, 0)
+        weave_w3(on_scalar, 1, 1, 1, SIDE // VECTOR_SHARE, SIDE)
+        weave_w3(on_vector, 1, 1, 1, 0, SIDE // VECTOR_SHARE)
+        quantize_w3(1, 1)
+        y12_late = sbuf("y12_late", [P, HALF - EARLY, PACK], F32, over="w3_woven110")
+        nc.vector.tensor_tensor(y12_late[:], by_triple(1, 1)[:, EARLY:], y1[1][:, EARLY:], MULT)
         acc = [psum.tile([P, HALF], F32, name="acc%d" % h) for h in range(2)]
-        product(2)
-        warm_up(2, 1, 1, H)
+        product(LAST)
+        warm_up(LAST, 1)
 
+        parts = (
+            ((slice(0, HALF), y12_first),),
+            ((slice(0, EARLY), y12_early), (slice(EARLY, HALF), y12_late)),
+        )
         for h in range(2):
-            nc.vector.tensor_tensor(z[h][:], by_triple(2, h), y12[h][:], MULT)
+            for triples, y12 in parts[h]:
+                nc.vector.tensor_tensor(z[h][:, triples], by_triple(LAST, h)[:, triples], y12[:], MULT)
         for h in range(2):
-            nc.vector.quantize_mx(
-                out=z_codes[h][:].bitcast(FP8X4),
-                scales=z_scale[h][:],
-                in_=z[h][:].rearrange("p v t -> p (v t)"),
-            )
+            for triples, y12 in parts[h]:
+                nc.vector.quantize_mx(
+                    out=z_codes[h][:, triples].bitcast(FP8X4),
+                    scales=z_scale[h][:, triples],
+                    in_=z[h][:, triples].rearrange("p v t -> p (v t)"),
+                )
             nc.tensor.matmul_mx(
                 out=acc[h][:],
                 lhsT=w4_codes[:].bitcast(FP4X4),
@@ -266,7 +267,6 @@ def tile_picked_trilin_relu_e_kernel(tc, xT, w1, w2, w3, w4_words, w4_scales, of
                 stop=True,
             )
 
-        nc.scalar.activation(res[0][:], acc[0][:], RELU)
-        nc.sync.dma_start(out[:, 0:HALF], res[0][:])
-        nc.vector.tensor_scalar_max(res[1][:], acc[1][:], 0.0)
-        nc.sync.dma_start(out[:, HALF:V], res[1][:])
+        for h in range(2):
+            nc.vector.tensor_scalar_max(res[h][:], acc[h][:], 0.0)
+            nc.sync.dma_start(out[:, h * HALF : (h + 1) * HALF], res[h][:])

@@ -28,6 +28,7 @@ LIST_ROWS = 16
 RUN = 4
 SIDES = 2
 SIDE = P // SIDES
+BY_SIDES = ((2, 0), (2, 1))
 EARLY = HALF // 2
 VECTOR_SHARE = 4
 QUADRANT = 32
@@ -42,8 +43,11 @@ def tile_picked_trilin_relu_e_kernel(tc, xT, w1, w2, w3, w4_words, w4_scales, of
         keep = ctx.enter_context(tc.tile_pool(name="keep", bufs=1))
         psum = ctx.enter_context(tc.psum_pool(name="psum", bufs=1))
 
+        tags = {}
+
         def sbuf(name, shape, dtype, over=None):
-            return keep.tile(shape, dtype, name=name, tag=over or name, align_bytes=256)
+            tags[name] = tags[over] if over else name
+            return keep.tile(shape, dtype, name=name, tag=tags[name], align_bytes=256)
 
         offsets = keep.tile([P, S // LIST_ROWS], U16, name="offsets")
 
@@ -51,18 +55,29 @@ def tile_picked_trilin_relu_e_kernel(tc, xT, w1, w2, w3, w4_words, w4_scales, of
         for g in range(PASSES):
             rows = xT[g * K_PASS : (g + 1) * K_PASS, :].rearrange("(p j) c -> p j c", j=PACK)
             for j in range(PACK):
-                x_plane[g, j] = sbuf("x_plane%d%d" % (g, j), [P, T], F32)
-                nc.sync.dma_start(x_plane[g, j][:], rows[:, j, :])
                 if (g, j) == (0, 0):
+                    first_pair = sbuf("x_first_pair", [P, PAIR, T], F32)
+                    nc.sync.dma_start(first_pair[:], rows[:, 0:PAIR, :])
                     nc.sync.dma_start(offsets[:], offs)
-        w_raw, w3_raw = {}, {}
+                if g == 0 and j < PAIR:
+                    x_plane[g, j] = first_pair[:, j]
+                else:
+                    x_plane[g, j] = sbuf("x_plane%d%d" % (g, j), [P, T], F32)
+                    nc.sync.dma_start(x_plane[g, j][:], rows[:, j, :])
+        w_raw, side_raw, last_raw = {}, {}, {}
         for d in range(PIECES):
             for g in range(PASSES):
                 rows = weights[d][g * K_PASS : (g + 1) * K_PASS, :].rearrange("(p j) c -> p j c", j=PACK)
-                if d == LAST:
+                if (d, g) in BY_SIDES:
                     for a in range(SIDES):
-                        w3_raw[g, a] = sbuf("w3_raw%d%d" % (g, a), [P, PACK, H // SIDES], F32)
-                        nc.sync.dma_start(w3_raw[g, a][:], rows[:, :, a * H // SIDES : (a + 1) * H // SIDES])
+                        channels = rows[:, :, a * H // SIDES : (a + 1) * H // SIDES]
+                        if (g, a) == (PASSES - 1, SIDES - 1):
+                            for b in range(2):
+                                last_raw[b] = sbuf("last_raw%d" % b, [P, PACK, P], F32)
+                                nc.sync.dma_start(last_raw[b][:], channels[:, :, b * P : (b + 1) * P])
+                        else:
+                            side_raw[d, g, a] = sbuf("side_raw%d%d%d" % (d, g, a), [P, PACK, H // SIDES], F32)
+                            nc.sync.dma_start(side_raw[d, g, a][:], channels)
                 else:
                     w_raw[d, g] = sbuf("w_raw%d%d" % (d, g), [P, PACK, H], F32)
                     nc.sync.dma_start(w_raw[d, g][:], rows)
@@ -77,31 +92,39 @@ def tile_picked_trilin_relu_e_kernel(tc, xT, w1, w2, w3, w4_words, w4_scales, of
                 w4_scales[0, SCALE_ROWS * q : SCALE_ROWS * (q + 1), :].bitcast(I32),
             )
 
-        picked = {g: sbuf("picked%d" % g, [P, PACK, S], BF16) for g in range(PASSES)}
+        picked = {
+            0: sbuf("picked0", [P, PIECES, PACK, V], BF16),
+            1: sbuf("picked1", [P, PACK, PIECES, V], BF16)[:].rearrange("p j d v -> p d j v"),
+        }
         x_woven, x_codes, x_scale = {}, {}, {}
-        w_woven, w3_woven, w_codes, w_scale = {}, {}, {}, {}
+        x_both = (
+            sbuf("x_woven_both", [P, LAST * V, PACK], BF16),
+            sbuf("x_codes_both", [P, LAST * V], U32),
+            sbuf("x_scale_both", [P, LAST * V], U8),
+        )
+        w_woven, side_woven, w_codes, w_scale = {}, {}, {}, {}
         for d in range(PIECES):
             for g in range(PASSES):
-                x_woven[d, g] = sbuf("x_woven%d%d" % (d, g), [P, V, PACK], BF16)
-                x_codes[d, g] = sbuf("x_codes%d%d" % (d, g), [P, V], U32)
-                x_scale[d, g] = sbuf("x_scale%d%d" % (d, g), [P, V], U8)
-                for u in range(PACK // PAIR):
-                    if d == LAST:
-                        for a in range(SIDES):
-                            w3_woven[g, a, u] = sbuf("w3_woven%d%d%d" % (g, a, u), [P, PAIR, SIDE, PACK], BF16)
-                    else:
-                        w_woven[d, g, u] = sbuf("w_woven%d%d%d" % (d, g, u), [P, PAIR, P, PACK], BF16)
+                if g == 0 and d < LAST:
+                    entries = slice(d * V, (d + 1) * V)
+                    x_woven[d, g], x_codes[d, g], x_scale[d, g] = (both[:, entries] for both in x_both)
+                else:
+                    x_woven[d, g] = sbuf("x_woven%d%d" % (d, g), [P, V, PACK], BF16)
+                    x_codes[d, g] = sbuf("x_codes%d%d" % (d, g), [P, V], U32)
+                    x_scale[d, g] = sbuf("x_scale%d%d" % (d, g), [P, V], U8)
                 w_codes[d, g] = sbuf("w_codes%d%d" % (d, g), [P, H], U32)
                 w_scale[d, g] = sbuf("w_scale%d%d" % (d, g), [P, H], U8)
 
+        last_woven = {}
+
         def gather(g, j, first, end):
             entries = offsets[:, first // LIST_ROWS : end // LIST_ROWS]
-            nc.vector.tensor_copy(picked[g][:, j, first:end], x_plane[g, j][:].indirect(entries))
+            nc.vector.tensor_copy(picked[g][:, first // V : end // V, j], x_plane[g, j][:].indirect(entries))
 
         def weave_x(d, g):
             nc.scalar.copy(
                 x_woven[d, g][:].rearrange("p (c r) j -> p c j r", r=RUN),
-                picked[g][:, :, d * V : (d + 1) * V].rearrange("p j (c r) -> p c j r", r=RUN),
+                picked[g][:, d].rearrange("p j (c r) -> p c j r", r=RUN),
             )
 
         def quantize_x(d, g):
@@ -111,7 +134,9 @@ def tile_picked_trilin_relu_e_kernel(tc, xT, w1, w2, w3, w4_words, w4_scales, of
                 in_=x_woven[d, g][:].rearrange("p v j -> p (v j)"),
             )
 
-        def weave_w(copy, d, g, u, first=0, end=P):
+        def weave_w(copy, d, g, u, first=0, end=P, over=None):
+            if (d, g, u) not in w_woven:
+                w_woven[d, g, u] = sbuf("w_woven%d%d%d" % (d, g, u), [P, PAIR, P, PACK], BF16, over)
             copy(
                 w_woven[d, g, u][:, :, first:end].rearrange("p t m j -> p m j t"),
                 w_raw[d, g][:].rearrange("p j (m t) -> p m j t", t=PACK)[:, first:end, :, PAIR * u : PAIR * (u + 1)],
@@ -125,19 +150,30 @@ def tile_picked_trilin_relu_e_kernel(tc, xT, w1, w2, w3, w4_words, w4_scales, of
                 in_=w_woven[d, g, u][:, first - PAIR * u : end - PAIR * u, :, :].rearrange("p t m j -> p (t m j)"),
             )
 
-        def weave_w3(copy, g, a, u, first=0, end=SIDE):
+        def weave_side(copy, d, g, a, u, first=0, end=SIDE, over=None):
+            if (d, g, a, u) not in side_woven:
+                name = "side_woven%d%d%d%d" % (d, g, a, u)
+                side_woven[d, g, a, u] = sbuf(name, [P, PAIR, SIDE, PACK], BF16, over)
             copy(
-                w3_woven[g, a, u][:, :, first:end].rearrange("p t m j -> p m j t"),
-                w3_raw[g, a][:].rearrange("p j (m t) -> p m j t", t=PACK)[:, first:end, :, PAIR * u : PAIR * (u + 1)],
+                side_woven[d, g, a, u][:, :, first:end].rearrange("p t m j -> p m j t"),
+                side_raw[d, g, a][:].rearrange("p j (m t) -> p m j t", t=PACK)[:, first:end, :, PAIR * u : PAIR * (u + 1)],
             )
 
-        def quantize_w3(g, a):
-            for t in range(PACK):
+        def weave_last(copy, b, u, first=0, end=SIDE // 2):
+            if u not in last_woven:
+                last_woven[u] = side_woven[LAST, 1, 1, u] = sbuf("side_woven211%d" % u, [P, PAIR, SIDE, PACK], BF16)
+            copy(
+                last_woven[u][:, :, b * SIDE // 2 + first : b * SIDE // 2 + end].rearrange("p t m j -> p m j t"),
+                last_raw[b][:].rearrange("p j (m t) -> p m j t", t=PACK)[:, first:end, :, PAIR * u : PAIR * (u + 1)],
+            )
+
+        def quantize_side(d, g, a, first=0, end=PACK):
+            for t in range(first, end):
                 columns = slice(t * P + a * SIDE, t * P + (a + 1) * SIDE)
                 nc.vector.quantize_mx(
-                    out=w_codes[LAST, g][:, columns].bitcast(FP8X4),
-                    scales=w_scale[LAST, g][:, columns],
-                    in_=w3_woven[g, a, t // PAIR][:, t % PAIR, :, :].rearrange("p m j -> p (m j)"),
+                    out=w_codes[d, g][:, columns].bitcast(FP8X4),
+                    scales=w_scale[d, g][:, columns],
+                    in_=side_woven[d, g, a, t // PAIR][:, t % PAIR, :, :].rearrange("p m j -> p (m j)"),
                 )
 
         def warm_up(d, g):
@@ -179,17 +215,24 @@ def tile_picked_trilin_relu_e_kernel(tc, xT, w1, w2, w3, w4_words, w4_scales, of
         z_scale = [sbuf("z_scale%d" % h, [P, HALF], U8) for h in range(2)]
         res = [sbuf("res%d" % h, [P, HALF], F32) for h in range(2)]
 
-        for j in range(PACK):
-            gather(0, j, 0, S)
+        rounded = sbuf("rounded", [P, T], BF16)
+        nc.scalar.copy(rounded[:], x_plane[0, 1])
+        nc.scalar.activation(picked[0][:, :, 1], rounded[:].indirect(offsets[:]), mybir.ActivationFunctionType.Copy)
+        gather(0, 0, 0, S)
+        gather(0, 2, 0, S)
         for d in range(PIECES):
+            gather(0, PACK - 1, d * V, (d + 1) * V)
             weave_x(d, 0)
-        for j, d in zip(range(PACK - 1), range(PIECES)):
-            gather(1, j, 0, S)
-            quantize_x(d, 0)
+        gather(1, 0, 0, S)
+        nc.vector.quantize_mx(
+            out=x_both[1][:].bitcast(FP8X4), scales=x_both[2][:], in_=x_both[0][:].rearrange("p v j -> p (v j)")
+        )
+        quantize_x(LAST, 0)
+        gather(1, 1, 0, S)
+        gather(1, 2, 0, S)
         for d in range(PIECES):
             gather(1, PACK - 1, d * V, (d + 1) * V)
             weave_x(d, 1)
-
         weave_w(on_vector, 0, 0, 0)
         weave_w(on_vector, 0, 0, 1)
         quantize_x(0, 1)
@@ -202,42 +245,43 @@ def tile_picked_trilin_relu_e_kernel(tc, xT, w1, w2, w3, w4_words, w4_scales, of
         quantize_x(2, 1)
         quantize_w(0, 1, PAIR, PACK)
         product(0)
-
         weave_w(on_vector, 1, 0, 0)
-        weave_w(on_scalar, 1, 0, 1)
+        weave_w(on_vector, 1, 0, 1, 0, P // VECTOR_SHARE)
+        weave_w(on_scalar, 1, 0, 1, P // VECTOR_SHARE, P)
         quantize_w(1, 0, 0, PAIR)
         quantize_w(1, 0, PAIR, PACK)
-        y1 = [sbuf("y1_%d" % h, [P, HALF, PACK], F32, over="w_raw1%d" % h) for h in range(2)]
+        y1_both = sbuf("y1", [P, 2, HALF, PACK], F32, over="w_raw10")
+        y1 = [y1_both[:, h] for h in range(2)]
         nc.scalar.copy(y1[0][:], by_triple(0, 0))
+        nc.scalar.copy(y1[1][:], by_triple(0, 1))
         weave_w(on_vector, 1, 1, 0)
         weave_w(on_vector, 1, 1, 1, 0, P // VECTOR_SHARE)
         weave_w(on_scalar, 1, 1, 1, P // VECTOR_SHARE, P)
-        nc.scalar.copy(y1[1][:], by_triple(0, 1))
         for t in range(PACK):
             quantize_w(1, 1, t, t + 1)
         product(1)
-
         y12_first = sbuf("y12_first", [P, HALF, PACK], F32)
-        weave_w3(on_vector, 0, 0, 0)
-        weave_w3(on_scalar, 0, 0, 1)
+        weave_side(on_vector, LAST, 0, 0, 0)
+        weave_side(on_scalar, LAST, 0, 0, 1)
+        quantize_side(LAST, 0, 0)
         nc.vector.tensor_tensor(y12_first[:], by_triple(1, 0), y1[0][:], MULT)
         warm = psum.tile([P, H], F32, name="warm", tag="y10")
         warm_up(1, 1)
         warm_up(1, 1)
-        quantize_w3(0, 0)
-        weave_w3(on_scalar, 0, 1, 0)
-        weave_w3(on_scalar, 0, 1, 1)
+        weave_side(on_scalar, LAST, 0, 1, 0)
+        weave_side(on_scalar, LAST, 0, 1, 1)
         y12_early = sbuf("y12_early", [P, EARLY, PACK], F32)
         nc.vector.tensor_tensor(y12_early[:], by_triple(1, 1)[:, :EARLY], y1[1][:, :EARLY], MULT)
-        weave_w3(on_vector, 1, 0, 0)
-        weave_w3(on_scalar, 1, 0, 1)
-        quantize_w3(0, 1)
-        quantize_w3(1, 0)
-        weave_w3(on_vector, 1, 1, 0)
-        weave_w3(on_scalar, 1, 1, 1, SIDE // VECTOR_SHARE, SIDE)
-        weave_w3(on_vector, 1, 1, 1, 0, SIDE // VECTOR_SHARE)
-        quantize_w3(1, 1)
-        y12_late = sbuf("y12_late", [P, HALF - EARLY, PACK], F32, over="w3_woven110")
+        weave_side(on_vector, LAST, 1, 0, 0)
+        weave_side(on_scalar, LAST, 1, 0, 1)
+        weave_last(on_scalar, 0, 0)
+        weave_last(on_scalar, 0, 1)
+        quantize_side(LAST, 0, 1)
+        quantize_side(LAST, 1, 0)
+        weave_last(on_vector, 1, 0)
+        weave_last(on_vector, 1, 1)
+        quantize_side(LAST, 1, 1)
+        y12_late = sbuf("y12_late", [P, HALF - EARLY, PACK], F32, over="side_woven2110")
         nc.vector.tensor_tensor(y12_late[:], by_triple(1, 1)[:, EARLY:], y1[1][:, EARLY:], MULT)
         acc = [psum.tile([P, HALF], F32, name="acc%d" % h) for h in range(2)]
         product(LAST)

@@ -29,7 +29,7 @@ RUN = 4
 SIDES = 2
 SIDE = P // SIDES
 BY_SIDES = ((2, 0), (2, 1))
-EARLY = HALF // 2
+EARLY = HALF // 4
 VECTOR_SHARE = 4
 QUADRANT = 32
 SCALE_ROWS = 4
@@ -289,13 +289,14 @@ def tile_picked_trilin_relu_e_kernel(tc, xT, w1, w2, w3, w4_words, w4_scales, of
 
         parts = (
             ((slice(0, HALF), y12_first),),
-            ((slice(0, EARLY), y12_early), (slice(EARLY, HALF), y12_late)),
+            ((slice(EARLY, HALF), y12_late), (slice(0, EARLY), y12_early)),
         )
+        runs = ((slice(0, HALF),), (slice(HALF // 2, HALF), slice(0, HALF // 2)))
         for h in range(2):
             for triples, y12 in parts[h]:
                 nc.vector.tensor_tensor(z[h][:, triples], by_triple(LAST, h)[:, triples], y12[:], MULT)
         for h in range(2):
-            for triples, y12 in parts[h]:
+            for triples in runs[h]:
                 nc.vector.quantize_mx(
                     out=z_codes[h][:, triples].bitcast(FP8X4),
                     scales=z_scale[h][:, triples],

@@ -176,13 +176,13 @@ def tile_picked_trilin_relu_e_kernel(tc, xT, w1, w2, w3, w4_words, w4_scales, of
                     in_=side_woven[d, g, a, t // PAIR][:, t % PAIR, :, :].rearrange("p m j -> p (m j)"),
                 )
 
-        def warm_up(d, g):
+        def warm_up(d, g, width):
             nc.tensor.matmul_mx(
-                out=warm[:],
+                out=warm[:, :width],
                 lhsT=w_codes[d, g][:, 0:P].bitcast(FP8X4),
                 lhsT_scale=w_scale[d, g][:, 0:P],
-                rhs=w_codes[d, g][:].bitcast(FP8X4),
-                rhs_scale=w_scale[d, g][:],
+                rhs=w_codes[d, g][:, :width].bitcast(FP8X4),
+                rhs_scale=w_scale[d, g][:, :width],
                 start=True,
                 stop=True,
             )
@@ -266,8 +266,8 @@ def tile_picked_trilin_relu_e_kernel(tc, xT, w1, w2, w3, w4_words, w4_scales, of
         quantize_side(LAST, 0, 0)
         nc.vector.tensor_tensor(y12_first[:], by_triple(1, 0), y1[0][:], MULT)
         warm = psum.tile([P, H], F32, name="warm", tag="y10")
-        warm_up(1, 1)
-        warm_up(1, 1)
+        warm_up(1, 1, H)
+        warm_up(1, 1, P)
         weave_side(on_scalar, LAST, 0, 1, 0)
         weave_side(on_scalar, LAST, 0, 1, 1)
         y12_early = sbuf("y12_early", [P, EARLY, PACK], F32)
@@ -285,7 +285,6 @@ def tile_picked_trilin_relu_e_kernel(tc, xT, w1, w2, w3, w4_words, w4_scales, of
         nc.vector.tensor_tensor(y12_late[:], by_triple(1, 1)[:, EARLY:], y1[1][:, EARLY:], MULT)
         acc = [psum.tile([P, HALF], F32, name="acc%d" % h) for h in range(2)]
         product(LAST)
-        warm_up(LAST, 1)
 
         parts = (
             ((slice(0, HALF), y12_first),),

@@ -116,6 +116,10 @@ def tile_picked_trilin_relu_e_kernel(tc, xT, w1, w2, w3, w4_words, w4_scales, of
                 w_scale[d, g] = sbuf("w_scale%d%d" % (d, g), [P, H], U8)
 
         last_woven = {}
+        whole_woven = [sbuf("whole_woven%d" % g, [P, PACK, SIDE, PACK], BF16) for g in range(PASSES)]
+        for u in range(2):
+            side_woven[LAST, 0, 1, u] = whole_woven[0][:, PAIR * u : PAIR * (u + 1)]
+            last_woven[u] = side_woven[LAST, 1, 1, u] = whole_woven[1][:, PAIR * u : PAIR * (u + 1)]
 
         def gather(g, j, first, end):
             entries = offsets[:, first // LIST_ROWS : end // LIST_ROWS]
@@ -160,11 +164,15 @@ def tile_picked_trilin_relu_e_kernel(tc, xT, w1, w2, w3, w4_words, w4_scales, of
             )
 
         def weave_last(copy, b, u, first=0, end=SIDE // 2):
-            if u not in last_woven:
-                last_woven[u] = side_woven[LAST, 1, 1, u] = sbuf("side_woven211%d" % u, [P, PAIR, SIDE, PACK], BF16)
             copy(
                 last_woven[u][:, :, b * SIDE // 2 + first : b * SIDE // 2 + end].rearrange("p t m j -> p m j t"),
                 last_raw[b][:].rearrange("p j (m t) -> p m j t", t=PACK)[:, first:end, :, PAIR * u : PAIR * (u + 1)],
+            )
+
+        def weave_whole(d, g, a, raw, first, end):
+            nc.scalar.copy(
+                whole_woven[g][:, :, first:end].rearrange("p t m j -> p m j t"),
+                raw[:].rearrange("p j (m t) -> p m j t", t=PACK),
             )
 
         def quantize_side(d, g, a, first=0, end=PACK):
@@ -268,20 +276,18 @@ def tile_picked_trilin_relu_e_kernel(tc, xT, w1, w2, w3, w4_words, w4_scales, of
         warm = psum.tile([P, H], F32, name="warm", tag="y10")
         warm_up(1, 1, H)
         warm_up(1, 1, P)
-        weave_side(on_scalar, LAST, 0, 1, 0)
-        weave_side(on_scalar, LAST, 0, 1, 1)
+        weave_whole(LAST, 0, 1, side_raw[LAST, 0, 1], 0, SIDE)
         y12_early = sbuf("y12_early", [P, EARLY, PACK], F32)
         nc.vector.tensor_tensor(y12_early[:], by_triple(1, 1)[:, :EARLY], y1[1][:, :EARLY], MULT)
         weave_side(on_vector, LAST, 1, 0, 0)
         weave_side(on_scalar, LAST, 1, 0, 1)
-        weave_last(on_scalar, 0, 0)
-        weave_last(on_scalar, 0, 1)
+        weave_whole(LAST, 1, 1, last_raw[0], 0, SIDE // 2)
         quantize_side(LAST, 0, 1)
         quantize_side(LAST, 1, 0)
         weave_last(on_vector, 1, 0)
         weave_last(on_vector, 1, 1)
         quantize_side(LAST, 1, 1)
-        y12_late = sbuf("y12_late", [P, HALF - EARLY, PACK], F32, over="side_woven2110")
+        y12_late = sbuf("y12_late", [P, HALF - EARLY, PACK], F32, over="last_raw1")
         nc.vector.tensor_tensor(y12_late[:], by_triple(1, 1)[:, EARLY:], y1[1][:, EARLY:], MULT)
         acc = [psum.tile([P, HALF], F32, name="acc%d" % h) for h in range(2)]
         product(LAST)

@@ -29,7 +29,7 @@ RUN = 4
 SIDES = 2
 SIDE = P // SIDES
 BY_SIDES = ((2, 0), (2, 1))
-EARLY = HALF // 4
+AHEAD = PAIR * (V + HALF)
 VECTOR_SHARE = 4
 QUADRANT = 32
 SCALE_ROWS = 4
@@ -65,6 +65,7 @@ def tile_picked_trilin_relu_e_kernel(tc, xT, w1, w2, w3, w4_words, w4_scales, of
                     x_plane[g, j] = sbuf("x_plane%d%d" % (g, j), [P, T], F32)
                     nc.sync.dma_start(x_plane[g, j][:], rows[:, j, :])
         w_raw, side_raw, last_raw = {}, {}, {}
+        shared = sbuf("shared", [P, AHEAD + H], F32)
         for d in range(PIECES):
             for g in range(PASSES):
                 rows = weights[d][g * K_PASS : (g + 1) * K_PASS, :].rearrange("(p j) c -> p j c", j=PACK)
@@ -73,7 +74,10 @@ def tile_picked_trilin_relu_e_kernel(tc, xT, w1, w2, w3, w4_words, w4_scales, of
                         channels = rows[:, :, a * H // SIDES : (a + 1) * H // SIDES]
                         if (g, a) == (PASSES - 1, SIDES - 1):
                             for b in range(2):
-                                last_raw[b] = sbuf("last_raw%d" % b, [P, PACK, P], F32)
+                                if b == 0:
+                                    last_raw[b] = sbuf("last_raw0", [P, PACK, P], F32)
+                                else:
+                                    last_raw[b] = shared[:, AHEAD:].rearrange("p (j c) -> p j c", j=PACK)
                                 nc.sync.dma_start(last_raw[b][:], channels[:, :, b * P : (b + 1) * P])
                         else:
                             side_raw[d, g, a] = sbuf("side_raw%d%d%d" % (d, g, a), [P, PACK, H // SIDES], F32)
@@ -169,10 +173,10 @@ def tile_picked_trilin_relu_e_kernel(tc, xT, w1, w2, w3, w4_words, w4_scales, of
                 last_raw[b][:].rearrange("p j (m t) -> p m j t", t=PACK)[:, first:end, :, PAIR * u : PAIR * (u + 1)],
             )
 
-        def weave_whole(d, g, a, raw, first, end):
-            nc.scalar.copy(
+        def weave_whole(copy, g, raw, base, first, end):
+            copy(
                 whole_woven[g][:, :, first:end].rearrange("p t m j -> p m j t"),
-                raw[:].rearrange("p j (m t) -> p m j t", t=PACK),
+                raw[:].rearrange("p j (m t) -> p m j t", t=PACK)[:, first - base : end - base],
             )
 
         def quantize_side(d, g, a, first=0, end=PACK):
@@ -195,7 +199,25 @@ def tile_picked_trilin_relu_e_kernel(tc, xT, w1, w2, w3, w4_words, w4_scales, of
                 stop=True,
             )
 
-        y = {(d, h): psum.tile([P, PACK, HALF], F32, name="y%d%d" % (d, h)) for d in range(PIECES) for h in range(2)}
+        y = {(LAST, h): psum.tile([P, PACK, HALF], F32, name="y%d%d" % (LAST, h)) for h in range(2)}
+        y_pair = {(d, u): psum.tile([P, PAIR, V], F32, name="y%d%d" % (d, u)) for d in range(LAST) for u in range(2)}
+
+        def product_by_pairs(d):
+            for g in range(PASSES):
+                for t in range(PACK):
+                    columns = slice(t * P, (t + 1) * P)
+                    nc.tensor.matmul_mx(
+                        out=y_pair[d, t // PAIR][:, t % PAIR, :],
+                        lhsT=w_codes[d, g][:, columns].bitcast(FP8X4),
+                        lhsT_scale=w_scale[d, g][:, columns],
+                        rhs=x_codes[d, g][:].bitcast(FP8X4),
+                        rhs_scale=x_scale[d, g][:],
+                        start=(g == 0 and t % PAIR == 0),
+                        stop=(g == PASSES - 1 and t % PAIR == PAIR - 1),
+                    )
+
+        def pair_by_triple(d, u):
+            return y_pair[d, u][:].rearrange("p t v -> p v t")
 
         def product(d):
             for g in range(PASSES):
@@ -252,54 +274,58 @@ def tile_picked_trilin_relu_e_kernel(tc, xT, w1, w2, w3, w4_words, w4_scales, of
         quantize_w(0, 1, 0, PAIR)
         quantize_x(2, 1)
         quantize_w(0, 1, PAIR, PACK)
-        product(0)
+        product_by_pairs(0)
         weave_w(on_vector, 1, 0, 0)
         weave_w(on_vector, 1, 0, 1, 0, P // VECTOR_SHARE)
         weave_w(on_scalar, 1, 0, 1, P // VECTOR_SHARE, P)
         quantize_w(1, 0, 0, PAIR)
         quantize_w(1, 0, PAIR, PACK)
-        y1_both = sbuf("y1", [P, 2, HALF, PACK], F32, over="w_raw10")
-        y1 = [y1_both[:, h] for h in range(2)]
-        nc.scalar.copy(y1[0][:], by_triple(0, 0))
-        nc.scalar.copy(y1[1][:], by_triple(0, 1))
+        y1 = sbuf("y1", [P, 2, V, PAIR], F32, over="w_raw10")
+        nc.scalar.copy(y1[:, 0], pair_by_triple(0, 0))
+        nc.scalar.copy(y1[:, 1], pair_by_triple(0, 1))
         weave_w(on_vector, 1, 1, 0)
         weave_w(on_vector, 1, 1, 1, 0, P // VECTOR_SHARE)
         weave_w(on_scalar, 1, 1, 1, P // VECTOR_SHARE, P)
         for t in range(PACK):
             quantize_w(1, 1, t, t + 1)
-        product(1)
-        y12_first = sbuf("y12_first", [P, HALF, PACK], F32)
-        weave_side(on_vector, LAST, 0, 0, 0)
+        product_by_pairs(1)
+        y12 = shared[:, : PACK * V].rearrange("p (u v t) -> p u v t", u=2, t=PAIR)
+        weave_side(on_vector, LAST, 0, 0, 0, 0, SIDE // 2)
+        weave_side(on_scalar, LAST, 0, 0, 0, SIDE // 2, SIDE)
         weave_side(on_scalar, LAST, 0, 0, 1)
         quantize_side(LAST, 0, 0)
-        nc.vector.tensor_tensor(y12_first[:], by_triple(1, 0), y1[0][:], MULT)
+
+        def multiply(u, triples):
+            nc.vector.tensor_tensor(y12[:, u, triples], pair_by_triple(1, u)[:, triples], y1[:, u, triples], MULT)
+
+        multiply(0, slice(0, V))
         warm = psum.tile([P, H], F32, name="warm", tag="y10")
         warm_up(1, 1, H)
         warm_up(1, 1, P)
-        weave_whole(LAST, 0, 1, side_raw[LAST, 0, 1], 0, SIDE)
-        y12_early = sbuf("y12_early", [P, EARLY, PACK], F32)
-        nc.vector.tensor_tensor(y12_early[:], by_triple(1, 1)[:, :EARLY], y1[1][:, :EARLY], MULT)
+        weave_whole(on_scalar, 0, side_raw[LAST, 0, 1], 0, 0, SIDE)
+        multiply(1, slice(0, HALF))
         weave_side(on_vector, LAST, 1, 0, 0)
         weave_side(on_scalar, LAST, 1, 0, 1)
-        weave_whole(LAST, 1, 1, last_raw[0], 0, SIDE // 2)
+        weave_whole(on_scalar, 1, last_raw[0], 0, 0, SIDE // 2)
         quantize_side(LAST, 0, 1)
         quantize_side(LAST, 1, 0)
         weave_last(on_vector, 1, 0)
         weave_last(on_vector, 1, 1)
         quantize_side(LAST, 1, 1)
-        y12_late = sbuf("y12_late", [P, HALF - EARLY, PACK], F32, over="last_raw1")
-        nc.vector.tensor_tensor(y12_late[:], by_triple(1, 1)[:, EARLY:], y1[1][:, EARLY:], MULT)
+        multiply(1, slice(HALF, V))
         acc = [psum.tile([P, HALF], F32, name="acc%d" % h) for h in range(2)]
         product(LAST)
 
-        parts = (
-            ((slice(0, HALF), y12_first),),
-            ((slice(EARLY, HALF), y12_late), (slice(0, EARLY), y12_early)),
-        )
         runs = ((slice(0, HALF),), (slice(HALF // 2, HALF), slice(0, HALF // 2)))
         for h in range(2):
-            for triples, y12 in parts[h]:
-                nc.vector.tensor_tensor(z[h][:, triples], by_triple(LAST, h)[:, triples], y12[:], MULT)
+            factor = y12[:, :, h * HALF : (h + 1) * HALF].rearrange("p u v t -> p v u t")
+            for triples in runs[h]:
+                nc.vector.tensor_tensor(
+                    z[h][:, triples].rearrange("p v (u t) -> p v u t", t=PAIR),
+                    by_triple(LAST, h)[:, triples].rearrange("p v (u t) -> p v u t", t=PAIR),
+                    factor[:, triples],
+                    MULT,
+                )
         for h in range(2):
             for triples in runs[h]:
                 nc.vector.quantize_mx(

@@ -16,6 +16,7 @@ U8 = mybir.dt.uint8
 FP8X4 = mybir.dt.float8_e4m3fn_x4
 FP4X4 = mybir.dt.float4_e2m1fn_x4
 MULT = mybir.AluOpType.mult
+COPY = mybir.ActivationFunctionType.Copy
 
 P = 128
 PACK = 4
@@ -26,13 +27,26 @@ HALF = V // 2
 PAIR = PACK // 2
 LIST_ROWS = 16
 RUN = 4
-SIDES = 2
-SIDE = P // SIDES
-BY_SIDES = ((2, 0), (2, 1))
+SIDE = P // 2
 AHEAD = PAIR * (V + HALF)
 VECTOR_SHARE = 4
 QUADRANT = 32
 SCALE_ROWS = 4
+GAP = 16
+ALL, LEFT, RIGHT = (0, P), (0, SIDE), (SIDE, P)
+ROWS, LOW, HIGH = (0, PACK), (0, PAIR), (PAIR, PACK)
+X_LOADS = ((0, 0, 2), (0, 2, 4), (1, 0, 2), (1, 2, 3), (1, 3, 4))
+W_LOADS = (
+    (0, 0, ROWS, ALL),
+    (0, 1, ROWS, ALL),
+    (1, 0, ROWS, ALL),
+    (1, 1, ROWS, ALL),
+    (2, 0, ROWS, LEFT),
+    (2, 0, ROWS, RIGHT),
+    (2, 1, ROWS, LEFT),
+    (2, 1, ROWS, (SIDE, SIDE + SIDE // 2)),
+    (2, 1, ROWS, (SIDE + SIDE // 2, P)),
+)
 
 
 def tile_picked_trilin_relu_e_kernel(tc, xT, w1, w2, w3, w4_words, w4_scales, offs, out):
@@ -51,40 +65,32 @@ def tile_picked_trilin_relu_e_kernel(tc, xT, w1, w2, w3, w4_words, w4_scales, of
 
         offsets = keep.tile([P, S // LIST_ROWS], U16, name="offsets")
 
+        def pass_rows(matrix, g):
+            return matrix[g * K_PASS : (g + 1) * K_PASS, :].rearrange("(p j) c -> p j c", j=PACK)
+
         x_plane = {}
-        for g in range(PASSES):
-            rows = xT[g * K_PASS : (g + 1) * K_PASS, :].rearrange("(p j) c -> p j c", j=PACK)
-            for j in range(PACK):
-                if (g, j) == (0, 0):
-                    first_pair = sbuf("x_first_pair", [P, PAIR, T], F32)
-                    nc.sync.dma_start(first_pair[:], rows[:, 0:PAIR, :])
-                    nc.sync.dma_start(offsets[:], offs)
-                if g == 0 and j < PAIR:
-                    x_plane[g, j] = first_pair[:, j]
-                else:
-                    x_plane[g, j] = sbuf("x_plane%d%d" % (g, j), [P, T], F32)
-                    nc.sync.dma_start(x_plane[g, j][:], rows[:, j, :])
-        w_raw, side_raw, last_raw = {}, {}, {}
+        for g, first, end in X_LOADS:
+            name = "x%d%d" % (g, first)
+            if end - first == 1:
+                x_plane[g, first] = sbuf(name, [P, T], F32)[:]
+                nc.sync.dma_start(x_plane[g, first], pass_rows(xT, g)[:, first, :])
+            else:
+                planes = sbuf(name, [P, end - first, T], F32)
+                nc.sync.dma_start(planes[:], pass_rows(xT, g)[:, first:end, :])
+                for j in range(first, end):
+                    x_plane[g, j] = planes[:, j - first]
+            if (g, first) == (0, 0):
+                nc.sync.dma_start(offsets[:], offs)
+
+        raw = {}
         shared = sbuf("shared", [P, AHEAD + H], F32)
-        for d in range(PIECES):
-            for g in range(PASSES):
-                rows = weights[d][g * K_PASS : (g + 1) * K_PASS, :].rearrange("(p j) c -> p j c", j=PACK)
-                if (d, g) in BY_SIDES:
-                    for a in range(SIDES):
-                        channels = rows[:, :, a * H // SIDES : (a + 1) * H // SIDES]
-                        if (g, a) == (PASSES - 1, SIDES - 1):
-                            for b in range(2):
-                                if b == 0:
-                                    last_raw[b] = sbuf("last_raw0", [P, PACK, P], F32)
-                                else:
-                                    last_raw[b] = shared[:, AHEAD:].rearrange("p (j c) -> p j c", j=PACK)
-                                nc.sync.dma_start(last_raw[b][:], channels[:, :, b * P : (b + 1) * P])
-                        else:
-                            side_raw[d, g, a] = sbuf("side_raw%d%d%d" % (d, g, a), [P, PACK, H // SIDES], F32)
-                            nc.sync.dma_start(side_raw[d, g, a][:], channels)
-                else:
-                    w_raw[d, g] = sbuf("w_raw%d%d" % (d, g), [P, PACK, H], F32)
-                    nc.sync.dma_start(w_raw[d, g][:], rows)
+        for load in W_LOADS:
+            d, g, (j0, j1), (m0, m1) = load
+            if load == W_LOADS[-1]:
+                raw[load] = shared[:, AHEAD:].rearrange("p (j c) -> p j c", j=j1 - j0)
+            else:
+                raw[load] = sbuf("raw%d%d%d%d" % (d, g, j0, m0), [P, j1 - j0, PACK * (m1 - m0)], F32)[:]
+            nc.sync.dma_start(raw[load], pass_rows(weights[d], g)[:, j0:j1, PACK * m0 : PACK * m1])
 
         w4_codes = sbuf("w4_codes", [P, 2 * N], U8)
         w4_scale = sbuf("w4_scale", [P, N], U8)
@@ -97,20 +103,20 @@ def tile_picked_trilin_relu_e_kernel(tc, xT, w1, w2, w3, w4_words, w4_scales, of
             )
 
         picked = {
-            0: sbuf("picked0", [P, PIECES, PACK, V], BF16),
-            1: sbuf("picked1", [P, PACK, PIECES, V], BF16)[:].rearrange("p j d v -> p d j v"),
+            0: sbuf("picked0", [P, PACK, 2 * PIECES, HALF + GAP], BF16),
+            1: sbuf("picked1", [P, PACK, 2 * PIECES, HALF + GAP], BF16),
         }
         x_woven, x_codes, x_scale = {}, {}, {}
+        w_codes, w_scale, woven = {}, {}, {}
         x_both = (
             sbuf("x_woven_both", [P, LAST * V, PACK], BF16),
             sbuf("x_codes_both", [P, LAST * V], U32),
             sbuf("x_scale_both", [P, LAST * V], U8),
         )
-        w_woven, side_woven, w_codes, w_scale = {}, {}, {}, {}
         for d in range(PIECES):
             for g in range(PASSES):
-                if g == 0 and d < LAST:
-                    entries = slice(d * V, (d + 1) * V)
+                if g == 0 and d > 0:
+                    entries = slice((d - 1) * V, d * V)
                     x_woven[d, g], x_codes[d, g], x_scale[d, g] = (both[:, entries] for both in x_both)
                 else:
                     x_woven[d, g] = sbuf("x_woven%d%d" % (d, g), [P, V, PACK], BF16)
@@ -119,20 +125,21 @@ def tile_picked_trilin_relu_e_kernel(tc, xT, w1, w2, w3, w4_words, w4_scales, of
                 w_codes[d, g] = sbuf("w_codes%d%d" % (d, g), [P, H], U32)
                 w_scale[d, g] = sbuf("w_scale%d%d" % (d, g), [P, H], U8)
 
-        last_woven = {}
-        whole_woven = [sbuf("whole_woven%d" % g, [P, PACK, SIDE, PACK], BF16) for g in range(PASSES)]
-        for u in range(2):
-            side_woven[LAST, 0, 1, u] = whole_woven[0][:, PAIR * u : PAIR * (u + 1)]
-            last_woven[u] = side_woven[LAST, 1, 1, u] = whole_woven[1][:, PAIR * u : PAIR * (u + 1)]
+        def picked_entries(g, j, first, end):
+            return picked[g][:, j, first // HALF : end // HALF, :HALF]
 
-        def gather(g, j, first, end):
+        def gather(g, j, first=0, end=S):
             entries = offsets[:, first // LIST_ROWS : end // LIST_ROWS]
-            nc.vector.tensor_copy(picked[g][:, first // V : end // V, j], x_plane[g, j][:].indirect(entries))
+            nc.vector.tensor_copy(picked_entries(g, j, first, end), x_plane[g, j].indirect(entries))
 
-        def weave_x(d, g):
-            nc.scalar.copy(
-                x_woven[d, g][:].rearrange("p (c r) j -> p c j r", r=RUN),
-                picked[g][:, d].rearrange("p j (c r) -> p c j r", r=RUN),
+        def gather_on_scalar(g, j, first=0, end=S):
+            entries = offsets[:, first // LIST_ROWS : end // LIST_ROWS]
+            nc.scalar.activation(picked_entries(g, j, first, end), x_plane[g, j].indirect(entries), COPY)
+
+        def weave_x(copy, d, g):
+            copy(
+                x_woven[d, g][:].rearrange("p (h c r) j -> p h c j r", h=2, r=RUN),
+                picked[g][:, :, 2 * d : 2 * d + 2, :HALF].rearrange("p j h (c r) -> p h c j r", r=RUN),
             )
 
         def quantize_x(d, g):
@@ -142,51 +149,38 @@ def tile_picked_trilin_relu_e_kernel(tc, xT, w1, w2, w3, w4_words, w4_scales, of
                 in_=x_woven[d, g][:].rearrange("p v j -> p (v j)"),
             )
 
-        def weave_w(copy, d, g, u, first=0, end=P, over=None):
-            if (d, g, u) not in w_woven:
-                w_woven[d, g, u] = sbuf("w_woven%d%d%d" % (d, g, u), [P, PAIR, P, PACK], BF16, over)
+        def woven_tile(d, g, side):
+            if (d, g, side) not in woven:
+                name = "woven%d%d%d" % (d, g, side[0])
+                woven[d, g, side] = sbuf(name, [P, PACK, side[1] - side[0], PACK], BF16)
+            return woven[d, g, side]
+
+        def weave(copy, load, t0, t1, first=None, end=None):
+            d, g, (j0, j1), (m0, m1) = load
+            side = ALL if (m0, m1) == ALL else LEFT if m0 < SIDE else RIGHT
+            first = m0 if first is None else first
+            end = m1 if end is None else end
             copy(
-                w_woven[d, g, u][:, :, first:end].rearrange("p t m j -> p m j t"),
-                w_raw[d, g][:].rearrange("p j (m t) -> p m j t", t=PACK)[:, first:end, :, PAIR * u : PAIR * (u + 1)],
+                woven_tile(d, g, side)[:, t0:t1, first - side[0] : end - side[0], j0:j1].rearrange("p t m j -> p m j t"),
+                raw[load].rearrange("p j (m t) -> p m j t", t=PACK)[:, first - m0 : end - m0, :, t0:t1],
             )
 
-        def quantize_w(d, g, first, end):
-            u = first // PAIR
-            nc.vector.quantize_mx(
-                out=w_codes[d, g][:, first * P : end * P].bitcast(FP8X4),
-                scales=w_scale[d, g][:, first * P : end * P],
-                in_=w_woven[d, g, u][:, first - PAIR * u : end - PAIR * u, :, :].rearrange("p t m j -> p (t m j)"),
-            )
-
-        def weave_side(copy, d, g, a, u, first=0, end=SIDE, over=None):
-            if (d, g, a, u) not in side_woven:
-                name = "side_woven%d%d%d%d" % (d, g, a, u)
-                side_woven[d, g, a, u] = sbuf(name, [P, PAIR, SIDE, PACK], BF16, over)
-            copy(
-                side_woven[d, g, a, u][:, :, first:end].rearrange("p t m j -> p m j t"),
-                side_raw[d, g, a][:].rearrange("p j (m t) -> p m j t", t=PACK)[:, first:end, :, PAIR * u : PAIR * (u + 1)],
-            )
-
-        def weave_last(copy, b, u, first=0, end=SIDE // 2):
-            copy(
-                last_woven[u][:, :, b * SIDE // 2 + first : b * SIDE // 2 + end].rearrange("p t m j -> p m j t"),
-                last_raw[b][:].rearrange("p j (m t) -> p m j t", t=PACK)[:, first:end, :, PAIR * u : PAIR * (u + 1)],
-            )
-
-        def weave_whole(copy, g, raw, base, first, end):
-            copy(
-                whole_woven[g][:, :, first:end].rearrange("p t m j -> p m j t"),
-                raw[:].rearrange("p j (m t) -> p m j t", t=PACK)[:, first - base : end - base],
-            )
-
-        def quantize_side(d, g, a, first=0, end=PACK):
-            for t in range(first, end):
-                columns = slice(t * P + a * SIDE, t * P + (a + 1) * SIDE)
+        def quantize_w(d, g, side, t0, t1):
+            if side == ALL:
+                columns = slice(t0 * P, t1 * P)
                 nc.vector.quantize_mx(
                     out=w_codes[d, g][:, columns].bitcast(FP8X4),
                     scales=w_scale[d, g][:, columns],
-                    in_=side_woven[d, g, a, t // PAIR][:, t % PAIR, :, :].rearrange("p m j -> p (m j)"),
+                    in_=woven[d, g, side][:, t0:t1].rearrange("p t m j -> p (t m j)"),
                 )
+            else:
+                for t in range(t0, t1):
+                    columns = slice(t * P + side[0], t * P + side[1])
+                    nc.vector.quantize_mx(
+                        out=w_codes[d, g][:, columns].bitcast(FP8X4),
+                        scales=w_scale[d, g][:, columns],
+                        in_=woven[d, g, side][:, t].rearrange("p m j -> p (m j)"),
+                    )
 
         def warm_up(d, g, width):
             nc.tensor.matmul_mx(
@@ -199,7 +193,7 @@ def tile_picked_trilin_relu_e_kernel(tc, xT, w1, w2, w3, w4_words, w4_scales, of
                 stop=True,
             )
 
-        y = {(LAST, h): psum.tile([P, PACK, HALF], F32, name="y%d%d" % (LAST, h)) for h in range(2)}
+        y = {h: psum.tile([P, PACK, HALF], F32, name="y2%d" % h) for h in range(2)}
         y_pair = {(d, u): psum.tile([P, PAIR, V], F32, name="y%d%d" % (d, u)) for d in range(LAST) for u in range(2)}
 
         def product_by_pairs(d):
@@ -219,7 +213,7 @@ def tile_picked_trilin_relu_e_kernel(tc, xT, w1, w2, w3, w4_words, w4_scales, of
         def pair_by_triple(d, u):
             return y_pair[d, u][:].rearrange("p t v -> p v t")
 
-        def product(d):
+        def last_product():
             for g in range(PASSES):
                 for h in range(2):
                     order = list(range(PACK)) if h == 0 else list(reversed(range(PACK)))
@@ -227,17 +221,14 @@ def tile_picked_trilin_relu_e_kernel(tc, xT, w1, w2, w3, w4_words, w4_scales, of
                     for t in order:
                         columns = slice(t * P, (t + 1) * P)
                         nc.tensor.matmul_mx(
-                            out=y[d, h][:, t, :],
-                            lhsT=w_codes[d, g][:, columns].bitcast(FP8X4),
-                            lhsT_scale=w_scale[d, g][:, columns],
-                            rhs=x_codes[d, g][:, triples].bitcast(FP8X4),
-                            rhs_scale=x_scale[d, g][:, triples],
+                            out=y[h][:, t, :],
+                            lhsT=w_codes[LAST, g][:, columns].bitcast(FP8X4),
+                            lhsT_scale=w_scale[LAST, g][:, columns],
+                            rhs=x_codes[LAST, g][:, triples].bitcast(FP8X4),
+                            rhs_scale=x_scale[LAST, g][:, triples],
                             start=(g == 0 and t == order[0]),
                             stop=(g == PASSES - 1 and t == order[-1]),
                         )
-
-        def by_triple(d, h):
-            return y[d, h][:].rearrange("p t v -> p v t")
 
         on_vector, on_scalar = nc.vector.tensor_copy, nc.scalar.copy
         z = [sbuf("z%d" % h, [P, HALF, PACK], BF16) for h in range(2)]
@@ -245,55 +236,55 @@ def tile_picked_trilin_relu_e_kernel(tc, xT, w1, w2, w3, w4_words, w4_scales, of
         z_scale = [sbuf("z_scale%d" % h, [P, HALF], U8) for h in range(2)]
         res = [sbuf("res%d" % h, [P, HALF], F32) for h in range(2)]
 
-        rounded = sbuf("rounded", [P, T], BF16)
-        nc.scalar.copy(rounded[:], x_plane[0, 1])
-        nc.scalar.activation(picked[0][:, :, 1], rounded[:].indirect(offsets[:]), mybir.ActivationFunctionType.Copy)
-        gather(0, 0, 0, S)
-        gather(0, 2, 0, S)
+        gather(0, 0)
+        gather(0, 1)
+        gather(0, 2)
         for d in range(PIECES):
-            gather(0, PACK - 1, d * V, (d + 1) * V)
-            weave_x(d, 0)
-        gather(1, 0, 0, S)
+            gather(0, 3, d * V, (d + 1) * V)
+            weave_x(on_scalar, d, 0)
+        quantize_x(0, 0)
+        gather(1, 0)
+        gather(1, 1)
         nc.vector.quantize_mx(
             out=x_both[1][:].bitcast(FP8X4), scales=x_both[2][:], in_=x_both[0][:].rearrange("p v j -> p (v j)")
         )
-        quantize_x(LAST, 0)
-        gather(1, 1, 0, S)
-        gather(1, 2, 0, S)
+        gather_on_scalar(1, 2)
         for d in range(PIECES):
-            gather(1, PACK - 1, d * V, (d + 1) * V)
-            weave_x(d, 1)
-        weave_w(on_vector, 0, 0, 0)
-        weave_w(on_vector, 0, 0, 1)
+            gather(1, 3, d * V, (d + 1) * V)
+            weave_x(on_scalar, d, 1)
+
+        w10, w11, w20, w21, w30a, w30b, w31, w31a, w31b = W_LOADS
+        weave(on_vector, w10, 0, 2)
+        weave(on_vector, w10, 2, 4)
         quantize_x(0, 1)
-        quantize_w(0, 0, 0, PAIR)
-        quantize_w(0, 0, PAIR, PACK)
-        weave_w(on_vector, 0, 1, 0)
-        weave_w(on_scalar, 0, 1, 1)
+        quantize_w(0, 0, ALL, 0, 2)
+        quantize_w(0, 0, ALL, 2, 4)
+        weave(on_vector, w11, 0, 2)
+        weave(on_scalar, w11, 2, 4)
         quantize_x(1, 1)
-        quantize_w(0, 1, 0, PAIR)
+        quantize_w(0, 1, ALL, 0, 2)
         quantize_x(2, 1)
-        quantize_w(0, 1, PAIR, PACK)
+        quantize_w(0, 1, ALL, 2, 4)
         product_by_pairs(0)
-        weave_w(on_vector, 1, 0, 0)
-        weave_w(on_vector, 1, 0, 1, 0, P // VECTOR_SHARE)
-        weave_w(on_scalar, 1, 0, 1, P // VECTOR_SHARE, P)
-        quantize_w(1, 0, 0, PAIR)
-        quantize_w(1, 0, PAIR, PACK)
-        y1 = sbuf("y1", [P, 2, V, PAIR], F32, over="w_raw10")
+        weave(on_vector, w20, 0, 2)
+        weave(on_vector, w20, 2, 4, 0, P // VECTOR_SHARE)
+        weave(on_scalar, w20, 2, 4, P // VECTOR_SHARE, P)
+        quantize_w(1, 0, ALL, 0, 2)
+        quantize_w(1, 0, ALL, 2, 4)
+        y1 = sbuf("y1", [P, 2, V, PAIR], F32, over="raw1000")
         nc.scalar.copy(y1[:, 0], pair_by_triple(0, 0))
         nc.scalar.copy(y1[:, 1], pair_by_triple(0, 1))
-        weave_w(on_vector, 1, 1, 0)
-        weave_w(on_vector, 1, 1, 1, 0, P // VECTOR_SHARE)
-        weave_w(on_scalar, 1, 1, 1, P // VECTOR_SHARE, P)
+        weave(on_vector, w21, 0, 2)
+        weave(on_vector, w21, 2, 4, 0, P // VECTOR_SHARE)
+        weave(on_scalar, w21, 2, 4, P // VECTOR_SHARE, P)
         for t in range(PACK):
-            quantize_w(1, 1, t, t + 1)
+            quantize_w(1, 1, ALL, t, t + 1)
         product_by_pairs(1)
         y12 = shared[:, : PACK * V].rearrange("p (u v t) -> p u v t", u=2, t=PAIR)
-        weave_side(on_vector, LAST, 0, 0, 0, 0, SIDE // 2)
-        weave_side(on_scalar, LAST, 0, 0, 0, SIDE // 2, SIDE)
-        weave_side(on_scalar, LAST, 0, 0, 1)
-        quantize_side(LAST, 0, 0)
+        weave(on_vector, w30a, 0, 2, 0, SIDE // 2)
+        weave(on_scalar, w30a, 0, 2, SIDE // 2, SIDE)
+        weave(on_scalar, w30a, 2, 4)
+        quantize_w(LAST, 0, LEFT, 0, 4)
 
         def multiply(u, triples):
             nc.vector.tensor_tensor(y12[:, u, triples], pair_by_triple(1, u)[:, triples], y1[:, u, triples], MULT)
@@ -302,19 +293,19 @@ def tile_picked_trilin_relu_e_kernel(tc, xT, w1, w2, w3, w4_words, w4_scales, of
         warm = psum.tile([P, H], F32, name="warm", tag="y10")
         warm_up(1, 1, H)
         warm_up(1, 1, P)
-        weave_whole(on_scalar, 0, side_raw[LAST, 0, 1], 0, 0, SIDE)
+        weave(on_scalar, w30b, 0, 4)
         multiply(1, slice(0, HALF))
-        weave_side(on_vector, LAST, 1, 0, 0)
-        weave_side(on_scalar, LAST, 1, 0, 1)
-        weave_whole(on_scalar, 1, last_raw[0], 0, 0, SIDE // 2)
-        quantize_side(LAST, 0, 1)
-        quantize_side(LAST, 1, 0)
-        weave_last(on_vector, 1, 0)
-        weave_last(on_vector, 1, 1)
-        quantize_side(LAST, 1, 1)
+        weave(on_vector, w31, 0, 2)
+        weave(on_scalar, w31, 2, 4)
+        weave(on_scalar, w31a, 0, 4)
+        quantize_w(LAST, 0, RIGHT, 0, 4)
+        quantize_w(LAST, 1, LEFT, 0, 4)
+        weave(on_vector, w31b, 0, 2)
+        weave(on_vector, w31b, 2, 4)
+        quantize_w(LAST, 1, RIGHT, 0, 4)
         multiply(1, slice(HALF, V))
         acc = [psum.tile([P, HALF], F32, name="acc%d" % h) for h in range(2)]
-        product(LAST)
+        last_product()
 
         runs = ((slice(0, HALF),), (slice(HALF // 2, HALF), slice(0, HALF // 2)))
         for h in range(2):
@@ -322,7 +313,7 @@ def tile_picked_trilin_relu_e_kernel(tc, xT, w1, w2, w3, w4_words, w4_scales, of
             for triples in runs[h]:
                 nc.vector.tensor_tensor(
                     z[h][:, triples].rearrange("p v (u t) -> p v u t", t=PAIR),
-                    by_triple(LAST, h)[:, triples].rearrange("p v (u t) -> p v u t", t=PAIR),
+                    y[h][:].rearrange("p (u t) v -> p v u t", t=PAIR)[:, triples],
                     factor[:, triples],
                     MULT,
                 )

@@ -95,7 +95,8 @@ def tile_picked_trilin_relu_e_kernel(tc, xT, w1, w2, w3, w4_words, w4_scales, of
         w4_codes = sbuf("w4_codes", [P, 2 * N], U8)
         w4_scale = sbuf("w4_scale", [P, N], U8)
         nc.vector.memset(w4_scale[:].bitcast(I32), 0)
-        nc.sync.dma_start(w4_codes[:].bitcast(I32), w4_words[0].bitcast(I32))
+        for first, end in ((0, N // 2), (N // 2, N), (N, 2 * N)):
+            nc.sync.dma_start(w4_codes[:, first:end].bitcast(I32), w4_words[0][:, first:end].bitcast(I32))
         for q in range(P // QUADRANT):
             nc.sync.dma_start(
                 w4_scale[QUADRANT * q : QUADRANT * q + SCALE_ROWS, :].bitcast(I32),

from contextlib import ExitStack

import concourse.mybir as mybir

K, T, V, H, N = 1024, 2048, 256, 512, 128
PIECES = 3
LAST = PIECES - 1
FLOPS = 2 * PIECES * K * H * V + 2 * H * N * V

F32 = mybir.dt.float32
BF16 = mybir.dt.bfloat16
I32 = mybir.dt.int32
U32 = mybir.dt.uint32
U16 = mybir.dt.uint16
U8 = mybir.dt.uint8
FP8X4 = mybir.dt.float8_e4m3fn_x4
FP4X4 = mybir.dt.float4_e2m1fn_x4
MULT = mybir.AluOpType.mult
COPY = mybir.ActivationFunctionType.Copy

P = 128
PACK = 4
K_PASS = P * PACK
PASSES = K // K_PASS
S = PIECES * V
HALF = V // 2
PAIR = PACK // 2
LIST_ROWS = 16
RUN = 4
SIDE = P // 2
AHEAD = PAIR * (V + HALF)
VECTOR_SHARE = 4
QUADRANT = 32
SCALE_ROWS = 4
GAP = 16
ALL, LEFT, RIGHT = (0, P), (0, SIDE), (SIDE, P)
ROWS, LOW, HIGH = (0, PACK), (0, PAIR), (PAIR, PACK)
X_LOADS = ((0, 0, 2), (0, 2, 4), (1, 0, 2), (1, 2, 3), (1, 3, 4))
W_LOADS = (
    (0, 0, ROWS, ALL),
    (0, 1, ROWS, ALL),
    (1, 0, ROWS, ALL),
    (1, 1, ROWS, ALL),
    (2, 0, ROWS, LEFT),
    (2, 0, ROWS, RIGHT),
    (2, 1, ROWS, LEFT),
    (2, 1, ROWS, (SIDE, SIDE + SIDE // 2)),
    (2, 1, ROWS, (SIDE + SIDE // 2, P)),
)


def tile_picked_trilin_relu_e_kernel(tc, xT, w1, w2, w3, w4_words, w4_scales, offs, out):
    nc = tc.nc
    weights = (w1, w2, w3)

    with ExitStack() as ctx:
        keep = ctx.enter_context(tc.tile_pool(name="keep", bufs=1))
        psum = ctx.enter_context(tc.psum_pool(name="psum", bufs=1))

        tags = {}

        def sbuf(name, shape, dtype, over=None):
            tags[name] = tags[over] if over else name
            return keep.tile(shape, dtype, name=name, tag=tags[name], align_bytes=256)

        offsets = keep.tile([P, S // LIST_ROWS], U16, name="offsets")

        def pass_rows(matrix, g):
            return matrix[g * K_PASS : (g + 1) * K_PASS, :].rearrange("(p j) c -> p j c", j=PACK)

        x_plane = {}
        for g, first, end in X_LOADS:
            name = "x%d%d" % (g, first)
            if end - first == 1:
                x_plane[g, first] = sbuf(name, [P, T], F32)[:]
                nc.sync.dma_start(x_plane[g, first], pass_rows(xT, g)[:, first, :])
            else:
                planes = sbuf(name, [P, end - first, T], F32)
                nc.sync.dma_start(planes[:], pass_rows(xT, g)[:, first:end, :])
                for j in range(first, end):
                    x_plane[g, j] = planes[:, j - first]
            if (g, first) == (0, 0):
                nc.sync.dma_start(offsets[:], offs)

        raw = {}
        shared = sbuf("shared", [P, AHEAD + H], F32)
        for load in W_LOADS:
            d, g, (j0, j1), (m0, m1) = load
            if load == W_LOADS[-1]:
                raw[load] = shared[:, AHEAD:].rearrange("p (j c) -> p j c", j=j1 - j0)
            else:
                raw[load] = sbuf("raw%d%d%d%d" % (d, g, j0, m0), [P, j1 - j0, PACK * (m1 - m0)], F32)[:]
            nc.sync.dma_start(raw[load], pass_rows(weights[d], g)[:, j0:j1, PACK * m0 : PACK * m1])

        w4_codes = sbuf("w4_codes", [P, 2 * N], U8)
        w4_scale = sbuf("w4_scale", [P, N], U8)
        nc.vector.memset(w4_scale[:].bitcast(I32), 0)
        for first, end in ((0, N // 2), (N // 2, N), (N, 2 * N)):
            nc.sync.dma_start(w4_codes[:, first:end].bitcast(I32), w4_words[0][:, first:end].bitcast(I32))
        for q in range(P // QUADRANT):
            nc.sync.dma_start(
                w4_scale[QUADRANT * q : QUADRANT * q + SCALE_ROWS, :].bitcast(I32),
                w4_scales[0, SCALE_ROWS * q : SCALE_ROWS * (q + 1), :].bitcast(I32),
            )

        picked = {
            0: sbuf("picked0", [P, PACK, 2 * PIECES, HALF + GAP], BF16),
            1: sbuf("picked1", [P, PACK, 2 * PIECES, HALF + GAP], BF16),
        }
        x_woven, x_codes, x_scale = {}, {}, {}
        w_codes, w_scale, woven = {}, {}, {}
        x_both = (
            sbuf("x_woven_both", [P, LAST * V, PACK], BF16),
            sbuf("x_codes_both", [P, LAST * V], U32),
            sbuf("x_scale_both", [P, LAST * V], U8),
        )
        for d in range(PIECES):
            for g in range(PASSES):
                if g == 0 and d > 0:
                    entries = slice((d - 1) * V, d * V)
                    x_woven[d, g], x_codes[d, g], x_scale[d, g] = (both[:, entries] for both in x_both)
                else:
                    x_woven[d, g] = sbuf("x_woven%d%d" % (d, g), [P, V, PACK], BF16)
                    x_codes[d, g] = sbuf("x_codes%d%d" % (d, g), [P, V], U32)
                    x_scale[d, g] = sbuf("x_scale%d%d" % (d, g), [P, V], U8)
                w_codes[d, g] = sbuf("w_codes%d%d" % (d, g), [P, H], U32)
                w_scale[d, g] = sbuf("w_scale%d%d" % (d, g), [P, H], U8)

        def picked_entries(g, j, first, end):
            return picked[g][:, j, first // HALF : end // HALF, :HALF]

        def gather(g, j, first=0, end=S):
            entries = offsets[:, first // LIST_ROWS : end // LIST_ROWS]
            nc.vector.tensor_copy(picked_entries(g, j, first, end), x_plane[g, j].indirect(entries))

        def gather_on_scalar(g, j, first=0, end=S):
            entries = offsets[:, first // LIST_ROWS : end // LIST_ROWS]
            nc.scalar.activation(picked_entries(g, j, first, end), x_plane[g, j].indirect(entries), COPY)

        def weave_x(copy, d, g):
            copy(
                x_woven[d, g][:].rearrange("p (h c r) j -> p h c j r", h=2, r=RUN),
                picked[g][:, :, 2 * d : 2 * d + 2, :HALF].rearrange("p j h (c r) -> p h c j r", r=RUN),
            )

        def quantize_x(d, g):
            nc.vector.quantize_mx(
                out=x_codes[d, g][:].bitcast(FP8X4),
                scales=x_scale[d, g][:],
                in_=x_woven[d, g][:].rearrange("p v j -> p (v j)"),
            )

        def woven_tile(d, g, side):
            if (d, g, side) not in woven:
                name = "woven%d%d%d" % (d, g, side[0])
                woven[d, g, side] = sbuf(name, [P, PACK, side[1] - side[0], PACK], BF16)
            return woven[d, g, side]

        def weave(copy, load, t0, t1, first=None, end=None):
            d, g, (j0, j1), (m0, m1) = load
            side = ALL if (m0, m1) == ALL else LEFT if m0 < SIDE else RIGHT
            first = m0 if first is None else first
            end = m1 if end is None else end
            copy(
                woven_tile(d, g, side)[:, t0:t1, first - side[0] : end - side[0], j0:j1].rearrange("p t m j -> p m j t"),
                raw[load].rearrange("p j (m t) -> p m j t", t=PACK)[:, first - m0 : end - m0, :, t0:t1],
            )

        def quantize_w(d, g, side, t0, t1):
            if side == ALL:
                columns = slice(t0 * P, t1 * P)
                nc.vector.quantize_mx(
                    out=w_codes[d, g][:, columns].bitcast(FP8X4),
                    scales=w_scale[d, g][:, columns],
                    in_=woven[d, g, side][:, t0:t1].rearrange("p t m j -> p (t m j)"),
                )
            else:
                for t in range(t0, t1):
                    columns = slice(t * P + side[0], t * P + side[1])
                    nc.vector.quantize_mx(
                        out=w_codes[d, g][:, columns].bitcast(FP8X4),
                        scales=w_scale[d, g][:, columns],
                        in_=woven[d, g, side][:, t].rearrange("p m j -> p (m j)"),
                    )

        def warm_up(d, g, width):
            nc.tensor.matmul_mx(
                out=warm[:, :width],
                lhsT=w_codes[d, g][:, 0:P].bitcast(FP8X4),
                lhsT_scale=w_scale[d, g][:, 0:P],
                rhs=w_codes[d, g][:, :width].bitcast(FP8X4),
                rhs_scale=w_scale[d, g][:, :width],
                start=True,
                stop=True,
            )

        y = {h: psum.tile([P, PACK, HALF], F32, name="y2%d" % h) for h in range(2)}
        y_pair = {(d, u): psum.tile([P, PAIR, V], F32, name="y%d%d" % (d, u)) for d in range(LAST) for u in range(2)}

        def product_by_pairs(d):
            for g in range(PASSES):
                for t in range(PACK):
                    columns = slice(t * P, (t + 1) * P)
                    nc.tensor.matmul_mx(
                        out=y_pair[d, t // PAIR][:, t % PAIR, :],
                        lhsT=w_codes[d, g][:, columns].bitcast(FP8X4),
                        lhsT_scale=w_scale[d, g][:, columns],
                        rhs=x_codes[d, g][:].bitcast(FP8X4),
                        rhs_scale=x_scale[d, g][:],
                        start=(g == 0 and t % PAIR == 0),
                        stop=(g == PASSES - 1 and t % PAIR == PAIR - 1),
                    )

        def pair_by_triple(d, u):
            return y_pair[d, u][:].rearrange("p t v -> p v t")

        def last_product():
            for g in range(PASSES):
                for h in range(2):
                    order = list(range(PACK)) if h == 0 else list(reversed(range(PACK)))
                    triples = slice(h * HALF, (h + 1) * HALF)
                    for t in order:
                        columns = slice(t * P, (t + 1) * P)
                        nc.tensor.matmul_mx(
                            out=y[h][:, t, :],
                            lhsT=w_codes[LAST, g][:, columns].bitcast(FP8X4),
                            lhsT_scale=w_scale[LAST, g][:, columns],
                            rhs=x_codes[LAST, g][:, triples].bitcast(FP8X4),
                            rhs_scale=x_scale[LAST, g][:, triples],
                            start=(g == 0 and t == order[0]),
                            stop=(g == PASSES - 1 and t == order[-1]),
                        )

        on_vector, on_scalar = nc.vector.tensor_copy, nc.scalar.copy
        z = [sbuf("z%d" % h, [P, HALF, PACK], BF16) for h in range(2)]
        z_codes = [sbuf("z_codes%d" % h, [P, HALF], U32) for h in range(2)]
        z_scale = [sbuf("z_scale%d" % h, [P, HALF], U8) for h in range(2)]
        res = [sbuf("res%d" % h, [P, HALF], F32) for h in range(2)]

        gather(0, 0)
        gather(0, 1)
        gather(0, 2)
        for d in range(PIECES):
            gather(0, 3, d * V, (d + 1) * V)
            weave_x(on_scalar, d, 0)
        quantize_x(0, 0)
        gather(1, 0)
        gather(1, 1)
        nc.vector.quantize_mx(
            out=x_both[1][:].bitcast(FP8X4), scales=x_both[2][:], in_=x_both[0][:].rearrange("p v j -> p (v j)")
        )
        gather_on_scalar(1, 2)
        for d in range(PIECES):
            gather(1, 3, d * V, (d + 1) * V)
            weave_x(on_scalar, d, 1)

        w10, w11, w20, w21, w30a, w30b, w31, w31a, w31b = W_LOADS
        weave(on_vector, w10, 0, 2)
        weave(on_vector, w10, 2, 4)
        quantize_x(0, 1)
        quantize_w(0, 0, ALL, 0, 2)
        quantize_w(0, 0, ALL, 2, 4)
        weave(on_vector, w11, 0, 2)
        weave(on_scalar, w11, 2, 4)
        quantize_x(1, 1)
        quantize_w(0, 1, ALL, 0, 2)
        quantize_x(2, 1)
        quantize_w(0, 1, ALL, 2, 4)
        product_by_pairs(0)
        weave(on_vector, w20, 0, 2)
        weave(on_vector, w20, 2, 4, 0, P // VECTOR_SHARE)
        weave(on_scalar, w20, 2, 4, P // VECTOR_SHARE, P)
        quantize_w(1, 0, ALL, 0, 2)
        quantize_w(1, 0, ALL, 2, 4)
        y1 = sbuf("y1", [P, 2, V, PAIR], F32, over="raw1000")
        nc.scalar.copy(y1[:, 0], pair_by_triple(0, 0))
        nc.scalar.copy(y1[:, 1], pair_by_triple(0, 1))
        weave(on_vector, w21, 0, 2)
        weave(on_vector, w21, 2, 4, 0, P // VECTOR_SHARE)
        weave(on_scalar, w21, 2, 4, P // VECTOR_SHARE, P)
        for t in range(PACK):
            quantize_w(1, 1, ALL, t, t + 1)
        product_by_pairs(1)
        y12 = shared[:, : PACK * V].rearrange("p (u v t) -> p u v t", u=2, t=PAIR)
        weave(on_vector, w30a, 0, 2, 0, SIDE // 2)
        weave(on_scalar, w30a, 0, 2, SIDE // 2, SIDE)
        weave(on_scalar, w30a, 2, 4)
        quantize_w(LAST, 0, LEFT, 0, 4)

        def multiply(u, triples):
            nc.vector.tensor_tensor(y12[:, u, triples], pair_by_triple(1, u)[:, triples], y1[:, u, triples], MULT)

        multiply(0, slice(0, V))
        warm = psum.tile([P, H], F32, name="warm", tag="y10")
        warm_up(1, 1, H)
        warm_up(1, 1, P)
        weave(on_scalar, w30b, 0, 4)
        multiply(1, slice(0, HALF))
        weave(on_vector, w31, 0, 2)
        weave(on_scalar, w31, 2, 4)
        weave(on_scalar, w31a, 0, 4)
        quantize_w(LAST, 0, RIGHT, 0, 4)
        quantize_w(LAST, 1, LEFT, 0, 4)
        weave(on_vector, w31b, 0, 2)
        weave(on_vector, w31b, 2, 4)
        quantize_w(LAST, 1, RIGHT, 0, 4)
        multiply(1, slice(HALF, V))
        acc = [psum.tile([P, HALF], F32, name="acc%d" % h) for h in range(2)]
        last_product()

        runs = ((slice(0, HALF),), (slice(HALF // 2, HALF), slice(0, HALF // 2)))
        for h in range(2):
            factor = y12[:, :, h * HALF : (h + 1) * HALF].rearrange("p u v t -> p v u t")
            for triples in runs[h]:
                nc.vector.tensor_tensor(
                    z[h][:, triples].rearrange("p v (u t) -> p v u t", t=PAIR),
                    y[h][:].rearrange("p (u t) v -> p v u t", t=PAIR)[:, triples],
                    factor[:, triples],
                    MULT,
                )
        for h in range(2):
            for triples in runs[h]:
                nc.vector.quantize_mx(
                    out=z_codes[h][:, triples].bitcast(FP8X4),
                    scales=z_scale[h][:, triples],
                    in_=z[h][:, triples].rearrange("p v t -> p (v t)"),
                )
            nc.tensor.matmul_mx(
                out=acc[h][:],
                lhsT=w4_codes[:].bitcast(FP4X4),
                lhsT_scale=w4_scale[:],
                rhs=z_codes[h][:].bitcast(FP8X4),
                rhs_scale=z_scale[h][:],
                start=True,
                stop=True,
            )

        for h in range(2):
            nc.vector.tensor_scalar_max(res[h][:], acc[h][:], 0.0)
            nc.sync.dma_start(out[:, h * HALF : (h + 1) * HALF], res[h][:])
